import numpy as np
import ml_dtypes


def mxq(x, axis, fmt="e4m3"):
    dtype, down = {"e4m3": (ml_dtypes.float8_e4m3fn, 7), "e5m2": (ml_dtypes.float8_e5m2, 14)}[fmt]
    v = np.moveaxis(np.asarray(x, np.float32).astype(ml_dtypes.bfloat16).astype(np.float64), axis, -1)
    blocks = v.reshape(v.shape[:-1] + (-1, 32))
    amax = np.abs(blocks).max(-1, keepdims=True)
    byte = np.maximum(np.where(amax > 0, np.frexp(amax)[1] - 1 + 127, 0) - down, 1)
    scale = np.exp2(byte - 127.0)
    codes = (blocks / scale).astype(np.float32).astype(dtype).astype(np.float64)
    return np.moveaxis((codes * scale).reshape(v.shape), -1, axis)


WIDE = False


def mx_kscale(k):
    if not WIDE:
        return np.ones(k)
    levels = np.array([10, -10, 5, -5, 0])
    if k % 512:
        return np.exp2(np.random.permutation(np.resize(levels, k // 32))).repeat(32)
    a = np.empty((k // 512, 16))
    for p in range(k // 512):
        a[p, :8] = np.random.permutation(np.resize(levels, 8))
        for g in range(8):
            far = levels[np.abs(levels - a[p, g]) >= 10]
            a[p, g + 8] = far[np.random.randint(len(far))]
    return np.exp2(a.ravel()).repeat(32)


BF16 = ml_dtypes.bfloat16


def bf(x):
    return np.asarray(x, np.float32).astype(BF16)


def f64(x):
    return np.asarray(x).astype(np.float64)


C, P, K = 1024, 1024, 1024


def draw0():
    s, t = mx_kscale(P), mx_kscale(K)
    return {"xa": bf(np.random.standard_normal((C, P)) * 2.0 * s),
            "xb": bf(np.random.standard_normal((C, P)) * 2.0 * s),
            "v": bf(np.random.standard_normal((P, K)) / np.sqrt(P) / s[:, None]),
            "ca": bf((1.0 + 0.1 * np.random.standard_normal(K)) * t),
            "cb": bf((1.0 + 0.1 * np.random.standard_normal(K)) / t)}


def whiten(xq, vq, scale):
    return (xq @ vq) * scale[None, :]


def core(xa, xb, v, ca, cb):
    n_channels = xa.shape[1]
    vq = mxq(f64(v), 0, "e4m3")

    a = whiten(mxq(f64(xa), 1, "e4m3"), vq, f64(ca))
    b = whiten(mxq(f64(xb), 1, "e4m3"), vq, f64(cb))

    gm = mxq(a, 1, "e4m3") @ mxq(b, 1, "e4m3").T

    e = np.sum(a * b, axis=1)

    return (e[:, None] + e[None, :] - gm - gm.T) / n_channels


def e4m3fn_bytes(y):
    return np.clip(np.asarray(y, np.float64), -448.0, 448.0).astype(np.float32).astype(ml_dtypes.float8_e4m3fn).view(np.uint8)


def e4m3fn_values(b):
    return np.asarray(b, np.uint8).view(ml_dtypes.float8_e4m3fn).astype(np.float64)


def setup_inputs():
    d = draw0()
    x0 = np.asarray(d['xb']).astype(np.float64)
    s = (np.max(np.abs(x0), axis=(0,), keepdims=True) / 448.0).astype(np.float32)
    out = {}
    for k, v in d.items():
        if k == 'xb':
            out['xb_bytes'] = e4m3fn_bytes(x0 / s.astype(np.float64))
            out['xb_scale'] = s
        else:
            out[k] = v
    return out


def reference(xa, xb_bytes, xb_scale, v, ca, cb):
    return core(xa, e4m3fn_values(xb_bytes) * xb_scale.astype(np.float64), v, ca, cb)

@@ -1,0 +1,386 @@
+from contextlib import ExitStack
+
+import concourse.mybir as mybir
+from concourse.masks import make_identity
+
+C, P, K = 1024, 1024, 1024
+FLOPS = 2 * C * P * K * 2 + 2 * C * C * K
+
+F32 = mybir.dt.float32
+BF16 = mybir.dt.bfloat16
+U32 = mybir.dt.uint32
+U8 = mybir.dt.uint8
+FP8 = mybir.dt.float8_e4m3fn
+FP8X4 = mybir.dt.float8_e4m3fn_x4
+ALU = mybir.AluOpType
+COPY = mybir.ActivationFunctionType.Copy
+
+PART = 128
+PACK = 4
+K_PASS = PART * PACK
+PASSES = P // K_PASS
+BANK = 512
+BANKS = 8
+HALF = C // 2
+PAIR = 2 * PART
+TILES = (2, 2, 2, 2)
+FIRST = [sum(TILES[:n]) for n in range(len(TILES) + 1)]
+CHUNKS = len(TILES)
+S_BANKS = 5
+
+
+def tile_crossnobisdissimilaritymatrix_kernel(tc, xa, xb_bytes, xb_scale, v, ca, cb, out):
+    nc = tc.nc
+    with ExitStack() as ctx:
+        keep = ctx.enter_context(tc.tile_pool(name="keep", bufs=1))
+        work = ctx.enter_context(tc.tile_pool(name="work", bufs=2))
+        psum = ctx.enter_context(tc.psum_pool(name="psum", bufs=1))
+        ctx.enter_context(tc.manual_schedule())
+
+        opened = {"scalar": [], "vector": []}
+        ring = {"scalar": S_BANKS, "vector": BANKS - S_BANKS}
+
+        def new_bank(shape, reader="scalar"):
+            tag = "%s_bank%d" % (reader, len(opened[reader]) % ring[reader])
+            opened[reader].append(tag)
+            return psum.tile(shape, F32, name=tag)
+
+        t = {}
+
+        def load_v(g, h):
+            raw = keep.tile([PART, PACK, K_PASS], BF16, name="v_raw_%d_%d" % (g, h))
+            rows = v[g * K_PASS:(g + 1) * K_PASS, h * K_PASS:(h + 1) * K_PASS]
+            nc.sync.dma_start(out=raw[:], in_=rows.rearrange("(p j) k -> p j k", j=PACK))
+            t["v_raw", g, h] = raw
+
+        def load_xa(m):
+            raw = keep.tile([PART, 2, P], BF16, name="xa_raw_%d" % m)
+            nc.sync.dma_start(out=raw[:], in_=xa[m * PAIR:(m + 1) * PAIR, :].rearrange("(i p) k -> p i k", p=PART))
+            for i in range(2):
+                t["x_rows", 0, 2 * m + i] = raw[:, i, :]
+
+        def load_xb(m):
+            raw = keep.tile([PART, 2, P], U8, name="xb_fp8_%d" % m)
+            nc.sync.dma_start(out=raw[:], in_=xb_bytes[m * PAIR:(m + 1) * PAIR, :].rearrange("(i p) k -> p i k", p=PART))
+            t["xb_fp8", m] = raw
+
+        factor_rows = keep.tile([PART, K // PACK], BF16, name="factor_rows")
+        ident = keep.tile([PART, PART], F32, name="ident")
+        nc.vector.memset(factor_rows[:], 0.0)
+        make_identity(nc, ident[:])
+
+        def load_scale():
+            nc.sync.dma_start(out=scale_cols[:], in_=xb_scale.rearrange("o (p i) -> (o p) i", p=PART))
+
+        def load_factors():
+            for i, factor in enumerate((ca, cb)):
+                nc.sync.dma_start(
+                    out=factor_rows[PACK * i:PACK * (i + 1), :].rearrange("t (b r) -> t b r", r=8),
+                    in_=factor.rearrange("(b t r) -> t b r", t=PACK, r=8))
+
+        scale_cols = keep.tile([PART, P // PART], F32, name="scale_cols")
+        scale_spread = keep.tile([PART, P], F32, name="scale_spread")
+        factor_f32 = keep.tile([PART, K // PACK], F32, name="factor_f32")
+        ca_cols = keep.tile([PART, PASSES, PACK], F32, name="ca_cols")
+        cb_cols = keep.tile([PART, PASSES, PACK], F32, name="cb_cols")
+        e_cols = keep.tile([PART, C // PART], F32, name="e_cols")
+
+        def spread_scale():
+            for half in range(P // BANK):
+                bank = new_bank([PART, PACK, PART])
+                for i in range(PACK):
+                    col = half * PACK + i
+                    nc.tensor.transpose(bank[:, i, :], scale_cols[:, col:col + 1].to_broadcast([PART, PART]), ident[:])
+                nc.scalar.activation(out=scale_spread[:].rearrange("p (m i) -> p m i", m=PART)[:, :, half * PACK:(half + 1) * PACK],
+                                     in_=bank[:].rearrange("p i m -> p m i"), func=COPY)
+
+        def turn_factors():
+            nc.scalar.copy(out=factor_f32[:], in_=factor_rows[:])
+            bank = new_bank([PART, PASSES, PART])
+            for h in range(PASSES):
+                nc.tensor.transpose(bank[:, h, :], factor_f32[:, h * PART:(h + 1) * PART], ident[:])
+            nc.scalar.activation(out=ca_cols[:], in_=bank[:, :, 0:PACK], func=COPY, scale=-1.0 / P)
+            nc.scalar.copy(out=cb_cols[:], in_=bank[:, :, PACK:2 * PACK])
+
+        def group_v(g, h, on_scalar):
+            grouped = work.tile([PART, PACK, PART * PACK], BF16, name="v_grouped", align_bytes=64, bufs=2)
+            cut = PACK - on_scalar
+            for slots, copy in ((slice(0, cut), nc.vector.tensor_copy), (slice(cut, PACK), nc.scalar.copy)):
+                if slots.start < slots.stop:
+                    copy(out=grouped[:, slots, :].rearrange("p t (q r j) -> p t q r j", r=8, j=PACK),
+                         in_=t["v_raw", g, h][:].rearrange("p j (q t r) -> p t q r j", t=PACK, r=8)[:, slots])
+            t["v_grouped", g, h] = grouped[:].rearrange("p t c -> p (t c)")
+
+        def quantize(name, key, grouped):
+            width = grouped.shape[1] // PACK
+            tag = name + "".join("_%d" % i for i in key)
+            codes = keep.tile([PART, width], U32, name=tag + "_codes", align_bytes=64)
+            scales = keep.tile([PART, width], U8, name=tag + "_scales", align_bytes=64)
+            nc.vector.quantize_mx(out=codes[:].bitcast(FP8X4), scales=scales[:], in_=grouped)
+            t[(name,) + key] = (codes, scales)
+
+        def quantize_v(g, h):
+            quantize("vq", (g, h), t["v_grouped", g, h])
+
+        def mx(acc, stationary, s_cols, moving, m_cols, start, stop):
+            nc.tensor.matmul_mx(
+                out=acc, lhsT=stationary[0][:, s_cols].bitcast(FP8X4), lhsT_scale=stationary[1][:, s_cols],
+                rhs=moving[0][:, m_cols].bitcast(FP8X4), rhs_scale=moving[1][:, m_cols], start=start, stop=stop)
+
+        def widen_xb(j):
+            rows = work.tile([PART, P], BF16, name="xb_rows", bufs=3)
+            nc.vector.tensor_tensor(out=rows[:], in0=t["xb_fp8", j // 2][:, j % 2, :].bitcast(FP8), in1=scale_spread[:], op=ALU.mult)
+            t["x_rows", 1, j] = rows[:]
+
+        def turn_x(run, m, g):
+            half, pair = divmod(m, 2)
+            if pair == 0:
+                t["x_grouped", run, half, g] = work.tile([PART, HALF * PACK], BF16, name="x_grouped", align_bytes=64, bufs=4)
+            bank = new_bank([PART, 2, PAIR])
+            for i in range(2):
+                words = t["x_rows", run, 2 * m + i].bitcast(F32)
+                for u in range(2):
+                    nc.tensor.transpose(bank[:, u, i * PART:(i + 1) * PART],
+                                        words[:, 256 * g + u:256 * (g + 1):2], ident[:])
+            cols = slice(pair * PAIR * PACK, (pair + 1) * PAIR * PACK)
+            nc.scalar.copy(out=t["x_grouped", run, half, g][:, cols].bitcast(F32).rearrange("p (c u) -> p c u", u=2),
+                           in_=bank[:].rearrange("p u c -> p c u"))
+
+        def quantize_x(run, half, g):
+            quantize("xq", (run, half, g), t["x_grouped", run, half, g][:])
+
+        def whiten(run, half, h):
+            white = work.tile([PART, PACK, HALF], F32, name="white", bufs=6)
+            for s in range(PACK):
+                bank = new_bank([PART, HALF])
+                for g in range(PASSES):
+                    mx(bank[:], t["vq", g, h], slice(s * PART, (s + 1) * PART), t["xq", run, half, g], slice(0, HALF),
+                       g == 0, g == PASSES - 1)
+                nc.scalar.activation(out=white[:, s, :], in_=bank[:], func=COPY, scale=(ca_cols, cb_cols)[run][:, h, s:s + 1])
+            t["white", run, half, h] = white
+
+        def white_cols(run, n, h):
+            half, c0 = divmod(FIRST[n] * PART, HALF)
+            return t["white", run, half, h][:, :, c0:c0 + TILES[n] * PART]
+
+        def group_ab(run, n, h, copy):
+            grouped = work.tile([PART, TILES[n] * PART, PACK], BF16, name="ab_grouped", align_bytes=64, bufs=4)
+            copy(out=grouped[:], in_=white_cols(run, n, h).rearrange("p s c -> p c s"))
+            t["ab_grouped", run, n, h] = grouped
+
+        abq = {}
+        for run in range(2):
+            for h in range(PASSES):
+                ab_codes = keep.tile([PART, C], U32, name="ab_codes_%d_%d" % (run, h), align_bytes=64)
+                ab_scales = keep.tile([PART, C], U8, name="ab_scales_%d_%d" % (run, h), align_bytes=64)
+                abq[run, h] = (ab_codes, ab_scales)
+
+        def quantize_ab(run, n, h):
+            cols = slice(FIRST[n] * PART, FIRST[n + 1] * PART)
+            codes, scales = abq[run, h]
+            nc.vector.quantize_mx(out=codes[:, cols].bitcast(FP8X4), scales=scales[:, cols],
+                                  in_=t["ab_grouped", run, n, h][:].rearrange("p c s -> p (c s)"))
+
+        def products(n, h):
+            prod = work.tile([PART, PACK, TILES[n] * PART], F32, name="prod", bufs=4)
+            nc.vector.tensor_tensor(out=prod[:], in0=white_cols(0, n, h), in1=white_cols(1, n, h), op=ALU.mult)
+            t["prod", n, h] = prod
+
+        def sum_products(n):
+            bank = new_bank([PART, TILES[n], PART], "vector")
+            for i in range(TILES[n]):
+                for h in range(PASSES):
+                    for s in range(PACK):
+                        nc.tensor.matmul(bank[:, i, :], lhsT=t["prod", n, h][:, s, i * PART:(i + 1) * PART], rhs=ident[:],
+                                         is_transpose=True, start=(h == 0 and s == 0), stop=(h == PASSES - 1 and s == PACK - 1))
+            t["e_bank", n] = bank
+
+        def reduce_e(n):
+            nc.vector.tensor_reduce(out=e_cols[:, FIRST[n]:FIRST[n + 1]], in_=t["e_bank", n][:], axis=mybir.AxisListType.X, op=ALU.add)
+
+        def spread_e(n):
+            bank = new_bank([PART, TILES[n], PART])
+            for i in range(TILES[n]):
+                col = FIRST[n] + i
+                nc.tensor.transpose(bank[:, i, :], e_cols[:, col:col + 1].to_broadcast([PART, PART]), ident[:])
+            nc.scalar.copy(out=e_spread[:, FIRST[n] * PART:FIRST[n + 1] * PART], in_=bank[:].rearrange("p i m -> p (i m)"))
+
+        e_spread = keep.tile([PART, C], F32, name="e_spread")
+
+        def gram(row, b):
+            c0, c1 = b * BANK, min((b + 1) * BANK, (row // 2 + 1) * PAIR)
+            bank = new_bank([PART, c1 - c0], "vector")
+            p0 = c0
+            for n_cols in (512, 256, 128):
+                if p0 + n_cols <= c1:
+                    for h in range(PASSES):
+                        for run in range(2):
+                            mx(bank[:, p0 - c0:p0 - c0 + n_cols], abq[run, h], slice(row * PART, (row + 1) * PART),
+                               abq[1 - run, h], slice(p0, p0 + n_cols), h == 0 and run == 0, h == PASSES - 1 and run == 1)
+                    p0 = p0 + n_cols
+            t["gram", row, b] = bank
+
+        def finish(row, b):
+            cols = slice(b * BANK, min((b + 1) * BANK, (row // 2 + 1) * PAIR))
+            rows = keep.tile([PART, cols.stop - cols.start], F32, name="rows_%d_%d" % (row, b))
+            nc.vector.scalar_tensor_tensor(out=rows[:], in0=t["gram", row, b][:], scalar=e_cols[:, row:row + 1],
+                                           in1=e_spread[:, cols], op0=ALU.subtract, op1=ALU.subtract)
+            nc.sync.dma_start(out=out[row * PART:(row + 1) * PART, cols], in_=rows[:])
+            t["rows", row, b] = rows
+
+        def mirror(rows, cols):
+            bank = new_bank([PART, len(cols), len(rows) * PART])
+            for j, col in enumerate(cols):
+                b, c0 = divmod(col * PART, BANK)
+                for i, row in enumerate(rows):
+                    nc.tensor.transpose(bank[:, j, i * PART:(i + 1) * PART], t["rows", row, b][:, c0:c0 + PART], ident[:])
+            mirrored = keep.tile([PART, len(cols), len(rows) * PART], F32, name="mirrored_%d_%d" % (rows[0], cols[0]))
+            nc.scalar.copy(out=mirrored[:], in_=bank[:])
+            target = out[cols[0] * PART:(cols[-1] + 1) * PART, rows[0] * PART:(rows[-1] + 1) * PART]
+            nc.sync.dma_start(out=target.rearrange("(j p) c -> p j c", p=PART), in_=mirrored[:])
+
+        on_v, on_s = nc.vector.tensor_copy, nc.scalar.copy
+        load_scale()
+        load_v(0, 0)
+        load_xb(0)
+        load_v(1, 0)
+        load_xb(1)
+        load_factors()
+        load_xa(0)
+        load_xa(1)
+        load_xb(2)
+        load_xb(3)
+        load_xa(2)
+        load_v(0, 1)
+        load_xa(3)
+        load_v(1, 1)
+        spread_scale()
+        group_v(0, 0, 2)
+        widen_xb(0)
+        widen_xb(1)
+        group_v(1, 0, 2)
+        turn_x(1, 0, 0)
+        turn_x(1, 0, 1)
+        widen_xb(2)
+        widen_xb(3)
+        turn_factors()
+        quantize_v(0, 0)
+        quantize_v(1, 0)
+        turn_x(1, 1, 0)
+        turn_x(1, 1, 1)
+        turn_x(0, 0, 0)
+        turn_x(0, 1, 0)
+        widen_xb(4)
+        quantize_x(1, 0, 0)
+        quantize_x(1, 0, 1)
+        turn_x(0, 0, 1)
+        turn_x(0, 1, 1)
+        widen_xb(5)
+        whiten(1, 0, 0)
+        quantize_x(0, 0, 0)
+        quantize_x(0, 0, 1)
+        turn_x(1, 2, 0)
+        turn_x(1, 2, 1)
+        turn_x(0, 2, 0)
+        turn_x(0, 2, 1)
+        widen_xb(6)
+        widen_xb(7)
+        whiten(0, 0, 0)
+        group_v(0, 1, 0)
+        turn_x(1, 3, 0)
+        turn_x(1, 3, 1)
+        group_v(1, 1, 0)
+        quantize_v(0, 1)
+        quantize_v(1, 1)
+        turn_x(0, 3, 0)
+        turn_x(0, 3, 1)
+        group_ab(1, 0, 0, on_v)
+        group_ab(1, 1, 0, on_v)
+        whiten(1, 0, 1)
+        quantize_x(1, 1, 0)
+        quantize_x(1, 1, 1)
+        products(0, 0)
+        products(1, 0)
+        whiten(0, 0, 1)
+        quantize_x(0, 1, 0)
+        quantize_x(0, 1, 1)
+        group_ab(0, 0, 0, on_v)
+        group_ab(0, 1, 0, on_v)
+        for run in (1, 0):
+            for n in (0, 1):
+                quantize_ab(run, n, 0)
+        whiten(1, 1, 0)
+        products(0, 1)
+        products(1, 1)
+        group_ab(0, 0, 1, on_s)
+        whiten(0, 1, 0)
+        group_ab(1, 0, 1, on_v)
+        group_ab(1, 1, 1, on_v)
+        group_ab(0, 1, 1, on_v)
+        sum_products(0)
+        sum_products(1)
+        for run in (1, 0):
+            for n in (0, 1):
+                quantize_ab(run, n, 1)
+        reduce_e(0)
+        reduce_e(1)
+        whiten(1, 1, 1)
+        spread_e(0)
+        spread_e(1)
+        products(3, 0)
+        group_ab(1, 3, 0, on_v)
+        group_ab(0, 3, 0, on_s)
+        gram(3, 0)
+        gram(2, 0)
+        products(2, 0)
+        finish(3, 0)
+        whiten(0, 1, 1)
+        finish(2, 0)
+        group_ab(1, 3, 1, on_v)
+        quantize_ab(1, 3, 0)
+        quantize_ab(0, 3, 0)
+        quantize_ab(1, 3, 1)
+        gram(1, 0)
+        gram(0, 0)
+        group_ab(0, 3, 1, on_s)
+        products(3, 1)
+        finish(1, 0)
+        finish(0, 0)
+        mirror((2, 3), (0, 1))
+        sum_products(3)
+        group_ab(0, 2, 0, on_s)
+        quantize_ab(0, 3, 1)
+        group_ab(1, 2, 0, on_v)
+        reduce_e(3)
+        products(2, 1)
+        gram(7, 0)
+        gram(6, 0)
+        group_ab(0, 2, 1, on_s)
+        group_ab(1, 2, 1, on_v)
+        quantize_ab(1, 2, 0)
+        quantize_ab(0, 2, 0)
+        finish(7, 0)
+        sum_products(2)
+        spread_e(3)
+        quantize_ab(1, 2, 1)
+        quantize_ab(0, 2, 1)
+        finish(6, 0)
+        reduce_e(2)
+        gram(5, 0)
+        gram(4, 0)
+        finish(5, 0)
+        mirror((6, 7), (0, 1))
+        mirror((6, 7), (2, 3))
+        spread_e(2)
+        finish(4, 0)
+        gram(7, 1)
+        gram(6, 1)
+        finish(7, 1)
+        mirror((4, 5), (0, 1))
+        mirror((4, 5), (2, 3))
+        finish(6, 1)
+        gram(5, 1)
+        mirror((6, 7), (4, 5))
+        gram(4, 1)
+        finish(5, 1)
+        finish(4, 1)

@@ -26,7 +26,6 @@ PAIR = 2 * PART
 TILES = (2, 2, 2, 2)
 FIRST = [sum(TILES[:n]) for n in range(len(TILES) + 1)]
 CHUNKS = len(TILES)
-S_BANKS = 5
 
 
 def tile_crossnobisdissimilaritymatrix_kernel(tc, xa, xb_bytes, xb_scale, v, ca, cb, out):
@@ -37,13 +36,12 @@ def tile_crossnobisdissimilaritymatrix_kernel(tc, xa, xb_bytes, xb_scale, v, ca,
         psum = ctx.enter_context(tc.psum_pool(name="psum", bufs=1))
         ctx.enter_context(tc.manual_schedule())
 
-        opened = {"scalar": [], "vector": []}
-        ring = {"scalar": S_BANKS, "vector": BANKS - S_BANKS}
+        opened = []
 
-        def new_bank(shape, reader="scalar"):
-            tag = "%s_bank%d" % (reader, len(opened[reader]) % ring[reader])
-            opened[reader].append(tag)
-            return psum.tile(shape, F32, name=tag)
+        def new_bank(shape, dtype=F32):
+            tag = "bank%d" % (len(opened) % BANKS)
+            opened.append(tag)
+            return psum.tile(shape, dtype, name=tag)
 
         t = {}
 
@@ -68,9 +66,11 @@ def tile_crossnobisdissimilaritymatrix_kernel(tc, xa, xb_bytes, xb_scale, v, ca,
         ident = keep.tile([PART, PART], F32, name="ident")
         nc.vector.memset(factor_rows[:], 0.0)
         make_identity(nc, ident[:])
+        ident_bf16 = keep.tile([PART, PART], BF16, name="ident_bf16")
+        make_identity(nc, ident_bf16[:])
 
         def load_scale():
-            nc.sync.dma_start(out=scale_cols[:], in_=xb_scale.rearrange("o (p i) -> (o p) i", p=PART))
+            nc.sync.dma_start(out=scale_cols[:].rearrange("p (b i) -> p b i", i=PACK), in_=xb_scale.rearrange("o (b p i) -> (o p) b i", p=PART, i=PACK))
 
         def load_factors():
             for i, factor in enumerate((ca, cb)):
@@ -80,7 +80,6 @@ def tile_crossnobisdissimilaritymatrix_kernel(tc, xa, xb_bytes, xb_scale, v, ca,
 
         scale_cols = keep.tile([PART, P // PART], F32, name="scale_cols")
         scale_spread = keep.tile([PART, P], F32, name="scale_spread")
-        factor_f32 = keep.tile([PART, K // PACK], F32, name="factor_f32")
         ca_cols = keep.tile([PART, PASSES, PACK], F32, name="ca_cols")
         cb_cols = keep.tile([PART, PASSES, PACK], F32, name="cb_cols")
         e_cols = keep.tile([PART, C // PART], F32, name="e_cols")
@@ -91,14 +90,13 @@ def tile_crossnobisdissimilaritymatrix_kernel(tc, xa, xb_bytes, xb_scale, v, ca,
                 for i in range(PACK):
                     col = half * PACK + i
                     nc.tensor.transpose(bank[:, i, :], scale_cols[:, col:col + 1].to_broadcast([PART, PART]), ident[:])
-                nc.scalar.activation(out=scale_spread[:].rearrange("p (m i) -> p m i", m=PART)[:, :, half * PACK:(half + 1) * PACK],
+                nc.scalar.activation(out=scale_spread[:, half * BANK:(half + 1) * BANK].rearrange("p (m i) -> p m i", i=PACK),
                                      in_=bank[:].rearrange("p i m -> p m i"), func=COPY)
 
         def turn_factors():
-            nc.scalar.copy(out=factor_f32[:], in_=factor_rows[:])
-            bank = new_bank([PART, PASSES, PART])
+            bank = new_bank([PART, PASSES, PART], dtype=BF16)
             for h in range(PASSES):
-                nc.tensor.transpose(bank[:, h, :], factor_f32[:, h * PART:(h + 1) * PART], ident[:])
+                nc.tensor.transpose(bank[:, h, :], factor_rows[:, h * PART:(h + 1) * PART], ident_bf16[:])
             nc.scalar.activation(out=ca_cols[:], in_=bank[:, :, 0:PACK], func=COPY, scale=-1.0 / P)
             nc.scalar.copy(out=cb_cols[:], in_=bank[:, :, PACK:2 * PACK])
 
@@ -107,8 +105,8 @@ def tile_crossnobisdissimilaritymatrix_kernel(tc, xa, xb_bytes, xb_scale, v, ca,
             cut = PACK - on_scalar
             for slots, copy in ((slice(0, cut), nc.vector.tensor_copy), (slice(cut, PACK), nc.scalar.copy)):
                 if slots.start < slots.stop:
-                    copy(out=grouped[:, slots, :].rearrange("p t (q r j) -> p t q r j", r=8, j=PACK),
-                         in_=t["v_raw", g, h][:].rearrange("p j (q t r) -> p t q r j", t=PACK, r=8)[:, slots])
+                    copy(out=grouped[:, slots, :].rearrange("p t (q r j) -> p t q j r", r=8, j=PACK),
+                         in_=t["v_raw", g, h][:].rearrange("p j (q t r) -> p t q j r", t=PACK, r=8)[:, slots])
             t["v_grouped", g, h] = grouped[:].rearrange("p t c -> p (t c)")
 
         def quantize(name, key, grouped):
@@ -128,7 +126,7 @@ def tile_crossnobisdissimilaritymatrix_kernel(tc, xa, xb_bytes, xb_scale, v, ca,
                 rhs=moving[0][:, m_cols].bitcast(FP8X4), rhs_scale=moving[1][:, m_cols], start=start, stop=stop)
 
         def widen_xb(j):
-            rows = work.tile([PART, P], BF16, name="xb_rows", bufs=3)
+            rows = work.tile([PART, P], BF16, name="xb_rows", bufs=4)
             nc.vector.tensor_tensor(out=rows[:], in0=t["xb_fp8", j // 2][:, j % 2, :].bitcast(FP8), in1=scale_spread[:], op=ALU.mult)
             t["x_rows", 1, j] = rows[:]
 
@@ -165,7 +163,8 @@ def tile_crossnobisdissimilaritymatrix_kernel(tc, xa, xb_bytes, xb_scale, v, ca,
 
         def group_ab(run, n, h, copy):
             grouped = work.tile([PART, TILES[n] * PART, PACK], BF16, name="ab_grouped", align_bytes=64, bufs=4)
-            copy(out=grouped[:], in_=white_cols(run, n, h).rearrange("p s c -> p c s"))
+            copy(out=grouped[:].rearrange("p (c i) s -> p c s i", i=4),
+                 in_=white_cols(run, n, h).rearrange("p s (c i) -> p c s i", i=4))
             t["ab_grouped", run, n, h] = grouped
 
         abq = {}
@@ -187,7 +186,7 @@ def tile_crossnobisdissimilaritymatrix_kernel(tc, xa, xb_bytes, xb_scale, v, ca,
             t["prod", n, h] = prod
 
         def sum_products(n):
-            bank = new_bank([PART, TILES[n], PART], "vector")
+            bank = new_bank([PART, TILES[n], PART])
             for i in range(TILES[n]):
                 for h in range(PASSES):
                     for s in range(PACK):
@@ -209,7 +208,7 @@ def tile_crossnobisdissimilaritymatrix_kernel(tc, xa, xb_bytes, xb_scale, v, ca,
 
         def gram(row, b):
             c0, c1 = b * BANK, min((b + 1) * BANK, (row // 2 + 1) * PAIR)
-            bank = new_bank([PART, c1 - c0], "vector")
+            bank = new_bank([PART, c1 - c0])
             p0 = c0
             for n_cols in (512, 256, 128):
                 if p0 + n_cols <= c1:
@@ -243,144 +242,144 @@ def tile_crossnobisdissimilaritymatrix_kernel(tc, xa, xb_bytes, xb_scale, v, ca,
         load_scale()
         load_v(0, 0)
         load_xb(0)
-        load_v(1, 0)
-        load_xb(1)
-        load_factors()
         load_xa(0)
+        load_factors()
+        load_xb(1)
+        load_v(1, 0)
         load_xa(1)
         load_xb(2)
-        load_xb(3)
         load_xa(2)
         load_v(0, 1)
         load_xa(3)
+        load_xb(3)
         load_v(1, 1)
         spread_scale()
         group_v(0, 0, 2)
+        turn_factors()
+        turn_x(0, 0, 0)
+        turn_x(0, 0, 1)
         widen_xb(0)
         widen_xb(1)
-        group_v(1, 0, 2)
         turn_x(1, 0, 0)
         turn_x(1, 0, 1)
         widen_xb(2)
         widen_xb(3)
-        turn_factors()
-        quantize_v(0, 0)
-        quantize_v(1, 0)
+        group_v(1, 0, 1)
+        turn_x(0, 1, 0)
+        turn_x(0, 1, 1)
         turn_x(1, 1, 0)
         turn_x(1, 1, 1)
-        turn_x(0, 0, 0)
-        turn_x(0, 1, 0)
-        widen_xb(4)
-        quantize_x(1, 0, 0)
-        quantize_x(1, 0, 1)
-        turn_x(0, 0, 1)
-        turn_x(0, 1, 1)
-        widen_xb(5)
-        whiten(1, 0, 0)
+        quantize_v(0, 0)
         quantize_x(0, 0, 0)
+        quantize_v(1, 0)
         quantize_x(0, 0, 1)
-        turn_x(1, 2, 0)
-        turn_x(1, 2, 1)
         turn_x(0, 2, 0)
         turn_x(0, 2, 1)
-        widen_xb(6)
-        widen_xb(7)
         whiten(0, 0, 0)
+        quantize_x(1, 0, 0)
+        quantize_x(1, 0, 1)
         group_v(0, 1, 0)
-        turn_x(1, 3, 0)
-        turn_x(1, 3, 1)
+        whiten(1, 0, 0)
         group_v(1, 1, 0)
         quantize_v(0, 1)
         quantize_v(1, 1)
         turn_x(0, 3, 0)
         turn_x(0, 3, 1)
-        group_ab(1, 0, 0, on_v)
-        group_ab(1, 1, 0, on_v)
-        whiten(1, 0, 1)
-        quantize_x(1, 1, 0)
-        quantize_x(1, 1, 1)
-        products(0, 0)
-        products(1, 0)
         whiten(0, 0, 1)
+        widen_xb(4)
+        widen_xb(5)
+        turn_x(1, 2, 0)
+        turn_x(1, 2, 1)
+        widen_xb(6)
+        widen_xb(7)
+        whiten(1, 0, 1)
         quantize_x(0, 1, 0)
         quantize_x(0, 1, 1)
+        turn_x(1, 3, 0)
+        turn_x(1, 3, 1)
+        products(0, 0)
+        products(1, 0)
+        whiten(0, 1, 0)
         group_ab(0, 0, 0, on_v)
+        quantize_x(1, 1, 0)
+        quantize_x(1, 1, 1)
         group_ab(0, 1, 0, on_v)
-        for run in (1, 0):
-            for n in (0, 1):
-                quantize_ab(run, n, 0)
         whiten(1, 1, 0)
         products(0, 1)
         products(1, 1)
-        group_ab(0, 0, 1, on_s)
-        whiten(0, 1, 0)
+        group_ab(1, 0, 0, on_v)
+        group_ab(1, 1, 0, on_v)
+        for run in (0, 1):
+            for n in (0, 1):
+                quantize_ab(run, n, 0)
+        whiten(0, 1, 1)
+        sum_products(0)
         group_ab(1, 0, 1, on_v)
         group_ab(1, 1, 1, on_v)
-        group_ab(0, 1, 1, on_v)
-        sum_products(0)
+        group_ab(0, 0, 1, on_v)
+        group_ab(0, 1, 1, on_s)
+        whiten(1, 1, 1)
         sum_products(1)
         for run in (1, 0):
             for n in (0, 1):
                 quantize_ab(run, n, 1)
         reduce_e(0)
+        products(2, 0)
+        group_ab(0, 2, 0, on_v)
+        group_ab(1, 2, 0, on_s)
+        group_ab(0, 2, 1, on_s)
+        group_ab(1, 2, 1, on_s)
+        gram(3, 0)
+        gram(2, 0)
         reduce_e(1)
-        whiten(1, 1, 1)
+        products(2, 1)
+        quantize_ab(0, 2, 0)
+        quantize_ab(1, 2, 0)
         spread_e(0)
         spread_e(1)
         products(3, 0)
-        group_ab(1, 3, 0, on_v)
-        group_ab(0, 3, 0, on_s)
-        gram(3, 0)
-        gram(2, 0)
-        products(2, 0)
-        finish(3, 0)
-        whiten(0, 1, 1)
-        finish(2, 0)
-        group_ab(1, 3, 1, on_v)
-        quantize_ab(1, 3, 0)
-        quantize_ab(0, 3, 0)
-        quantize_ab(1, 3, 1)
-        gram(1, 0)
-        gram(0, 0)
-        group_ab(0, 3, 1, on_s)
-        products(3, 1)
-        finish(1, 0)
-        finish(0, 0)
-        mirror((2, 3), (0, 1))
-        sum_products(3)
-        group_ab(0, 2, 0, on_s)
-        quantize_ab(0, 3, 1)
-        group_ab(1, 2, 0, on_v)
-        reduce_e(3)
-        products(2, 1)
-        gram(7, 0)
-        gram(6, 0)
-        group_ab(0, 2, 1, on_s)
-        group_ab(1, 2, 1, on_v)
-        quantize_ab(1, 2, 0)
-        quantize_ab(0, 2, 0)
-        finish(7, 0)
-        sum_products(2)
-        spread_e(3)
-        quantize_ab(1, 2, 1)
         quantize_ab(0, 2, 1)
-        finish(6, 0)
-        reduce_e(2)
+        quantize_ab(1, 2, 1)
+        sum_products(2)
+        group_ab(0, 3, 0, on_s)
+        group_ab(1, 3, 0, on_s)
+        finish(3, 0)
+        finish(2, 0)
         gram(5, 0)
+        reduce_e(2)
         gram(4, 0)
+        group_ab(0, 3, 1, on_s)
+        group_ab(1, 3, 1, on_s)
+        products(3, 1)
+        quantize_ab(0, 3, 0)
         finish(5, 0)
-        mirror((6, 7), (0, 1))
-        mirror((6, 7), (2, 3))
-        spread_e(2)
+        sum_products(3)
+        quantize_ab(1, 3, 0)
         finish(4, 0)
-        gram(7, 1)
-        gram(6, 1)
-        finish(7, 1)
+        quantize_ab(0, 3, 1)
+        reduce_e(3)
+        quantize_ab(1, 3, 1)
+        mirror((2, 3), (0, 1))
+        spread_e(2)
         mirror((4, 5), (0, 1))
         mirror((4, 5), (2, 3))
+        spread_e(3)
+        gram(7, 0)
+        gram(6, 0)
+        finish(7, 0)
+        gram(7, 1)
+        finish(6, 0)
+        gram(6, 1)
+        finish(7, 1)
+        mirror((6, 7), (0, 1))
+        mirror((6, 7), (2, 3))
         finish(6, 1)
         gram(5, 1)
         mirror((6, 7), (4, 5))
         gram(4, 1)
         finish(5, 1)
+        gram(1, 0)
         finish(4, 1)
+        gram(0, 0)
+        finish(1, 0)
+        finish(0, 0)

@@ -64,6 +64,8 @@ def tile_crossnobisdissimilaritymatrix_kernel(tc, xa, xb_bytes, xb_scale, v, ca,
 
         factor_rows = keep.tile([PART, K // PACK], BF16, name="factor_rows")
         ident = keep.tile([PART, PART], F32, name="ident")
+        warm_in = keep.tile([PART, BANK], BF16, name="warm_in")
+        nc.vector.memset(warm_in[:], 0.0)
         nc.vector.memset(factor_rows[:], 0.0)
         make_identity(nc, ident[:])
         ident_bf16 = keep.tile([PART, PART], BF16, name="ident_bf16")
@@ -238,6 +240,11 @@ def tile_crossnobisdissimilaritymatrix_kernel(tc, xa, xb_bytes, xb_scale, v, ca,
             target = out[cols[0] * PART:(cols[-1] + 1) * PART, rows[0] * PART:(rows[-1] + 1) * PART]
             nc.sync.dma_start(out=target.rearrange("(j p) c -> p j c", p=PART), in_=mirrored[:])
 
+        def warm(count):
+            bank = new_bank([PART, BANK])
+            for i in range(count):
+                nc.tensor.matmul(bank[:], lhsT=warm_in[:, 0:PART], rhs=warm_in[:], start=True, stop=True)
+
         on_v, on_s = nc.vector.tensor_copy, nc.scalar.copy
         load_scale()
         load_v(0, 0)
@@ -253,7 +260,9 @@ def tile_crossnobisdissimilaritymatrix_kernel(tc, xa, xb_bytes, xb_scale, v, ca,
         load_xa(3)
         load_xb(3)
         load_v(1, 1)
+        warm(4)
         spread_scale()
+        warm(7)
         group_v(0, 0, 2)
         turn_factors()
         turn_x(0, 0, 0)
@@ -265,10 +274,12 @@ def tile_crossnobisdissimilaritymatrix_kernel(tc, xa, xb_bytes, xb_scale, v, ca,
         widen_xb(2)
         widen_xb(3)
         group_v(1, 0, 1)
+        warm(3)
         turn_x(0, 1, 0)
         turn_x(0, 1, 1)
         turn_x(1, 1, 0)
         turn_x(1, 1, 1)
+        warm(2)
         quantize_v(0, 0)
         quantize_x(0, 0, 0)
         quantize_v(1, 0)

@@ -4,7 +4,7 @@ import concourse.mybir as mybir
 from concourse.masks import make_identity
 
 C, P, K = 1024, 1024, 1024
-FLOPS = 2 * C * P * K * 2 + 2 * C * C * K
+FLOPS = 2 * (2 * C * P * K) + 2 * C * C * K
 
 F32 = mybir.dt.float32
 BF16 = mybir.dt.bfloat16
@@ -16,26 +16,31 @@ ALU = mybir.AluOpType
 COPY = mybir.ActivationFunctionType.Copy
 
 PART = 128
-PACK = 4
-K_PASS = PART * PACK
+SLOTS = 4
+K_PASS = PART * SLOTS
 PASSES = P // K_PASS
+RUN_LEN = 8
+LINE = 4
 BANK = 512
 BANKS = 8
-HALF = C // 2
 PAIR = 2 * PART
-TILES = (2, 2, 2, 2)
-FIRST = [sum(TILES[:n]) for n in range(len(TILES) + 1)]
-CHUNKS = len(TILES)
+HALF = C // 2
+A, B = 0, 1
+
+V_SLOTS_ON_SCALAR = (2, 1)
+WARM_FIRST, WARM_SECOND, WARM_BETWEEN = 4, 7, 2
 
 
 def tile_crossnobisdissimilaritymatrix_kernel(tc, xa, xb_bytes, xb_scale, v, ca, cb, out):
     nc = tc.nc
+    on_vector, on_scalar = nc.vector.tensor_copy, nc.scalar.copy
     with ExitStack() as ctx:
         keep = ctx.enter_context(tc.tile_pool(name="keep", bufs=1))
         work = ctx.enter_context(tc.tile_pool(name="work", bufs=2))
         psum = ctx.enter_context(tc.psum_pool(name="psum", bufs=1))
         ctx.enter_context(tc.manual_schedule())
 
+        made = {}
         opened = []
 
         def new_bank(shape, dtype=F32):
@@ -43,26 +48,7 @@ def tile_crossnobisdissimilaritymatrix_kernel(tc, xa, xb_bytes, xb_scale, v, ca,
             opened.append(tag)
             return psum.tile(shape, dtype, name=tag)
 
-        t = {}
-
-        def load_v(g, h):
-            raw = keep.tile([PART, PACK, K_PASS], BF16, name="v_raw_%d_%d" % (g, h))
-            rows = v[g * K_PASS:(g + 1) * K_PASS, h * K_PASS:(h + 1) * K_PASS]
-            nc.sync.dma_start(out=raw[:], in_=rows.rearrange("(p j) k -> p j k", j=PACK))
-            t["v_raw", g, h] = raw
-
-        def load_xa(m):
-            raw = keep.tile([PART, 2, P], BF16, name="xa_raw_%d" % m)
-            nc.sync.dma_start(out=raw[:], in_=xa[m * PAIR:(m + 1) * PAIR, :].rearrange("(i p) k -> p i k", p=PART))
-            for i in range(2):
-                t["x_rows", 0, 2 * m + i] = raw[:, i, :]
-
-        def load_xb(m):
-            raw = keep.tile([PART, 2, P], U8, name="xb_fp8_%d" % m)
-            nc.sync.dma_start(out=raw[:], in_=xb_bytes[m * PAIR:(m + 1) * PAIR, :].rearrange("(i p) k -> p i k", p=PART))
-            t["xb_fp8", m] = raw
-
-        factor_rows = keep.tile([PART, K // PACK], BF16, name="factor_rows")
+        factor_rows = keep.tile([PART, K // SLOTS], BF16, name="factor_rows")
         ident = keep.tile([PART, PART], F32, name="ident")
         warm_in = keep.tile([PART, BANK], BF16, name="warm_in")
         nc.vector.memset(warm_in[:], 0.0)
@@ -71,181 +57,201 @@ def tile_crossnobisdissimilaritymatrix_kernel(tc, xa, xb_bytes, xb_scale, v, ca,
         ident_bf16 = keep.tile([PART, PART], BF16, name="ident_bf16")
         make_identity(nc, ident_bf16[:])
 
+        scale_cols = keep.tile([PART, P // PART], F32, name="scale_cols")
+        scale_spread = keep.tile([PART, P], F32, name="scale_spread")
+        ca_cols = keep.tile([PART, PASSES, SLOTS], F32, name="ca_cols")
+        cb_cols = keep.tile([PART, PASSES, SLOTS], F32, name="cb_cols")
+        e_cols = keep.tile([PART, C // PART], F32, name="e_cols")
+        e_spread = keep.tile([PART, C], F32, name="e_spread")
+        white_q = {}
+        for run in (A, B):
+            for h in range(PASSES):
+                white_codes = keep.tile([PART, C], U32, name="white_codes_%d_%d" % (run, h), align_bytes=64)
+                white_scales = keep.tile([PART, C], U8, name="white_scales_%d_%d" % (run, h), align_bytes=64)
+                white_q[run, h] = (white_codes, white_scales)
+
         def load_scale():
-            nc.sync.dma_start(out=scale_cols[:].rearrange("p (b i) -> p b i", i=PACK), in_=xb_scale.rearrange("o (b p i) -> (o p) b i", p=PART, i=PACK))
+            nc.sync.dma_start(out=scale_cols[:].rearrange("p (b i) -> p b i", i=SLOTS),
+                              in_=xb_scale.rearrange("o (b p i) -> (o p) b i", p=PART, i=SLOTS))
 
         def load_factors():
             for i, factor in enumerate((ca, cb)):
                 nc.sync.dma_start(
-                    out=factor_rows[PACK * i:PACK * (i + 1), :].rearrange("t (b r) -> t b r", r=8),
-                    in_=factor.rearrange("(b t r) -> t b r", t=PACK, r=8))
+                    out=factor_rows[SLOTS * i:SLOTS * (i + 1), :].rearrange("s (hq r) -> s hq r", r=RUN_LEN),
+                    in_=factor.rearrange("(hq s r) -> s hq r", s=SLOTS, r=RUN_LEN))
 
-        scale_cols = keep.tile([PART, P // PART], F32, name="scale_cols")
-        scale_spread = keep.tile([PART, P], F32, name="scale_spread")
-        ca_cols = keep.tile([PART, PASSES, PACK], F32, name="ca_cols")
-        cb_cols = keep.tile([PART, PASSES, PACK], F32, name="cb_cols")
-        e_cols = keep.tile([PART, C // PART], F32, name="e_cols")
+        def load_v(g, h):
+            raw = keep.tile([PART, SLOTS, K_PASS], BF16, name="v_raw_%d_%d" % (g, h))
+            quarter = v[g * K_PASS:(g + 1) * K_PASS, h * K_PASS:(h + 1) * K_PASS]
+            nc.sync.dma_start(out=raw[:], in_=quarter.rearrange("(p j) k -> p j k", j=SLOTS))
+            made["v_raw", g, h] = raw
+
+        def load_xa(pair):
+            raw = keep.tile([PART, 2, P], BF16, name="xa_raw_%d" % pair)
+            nc.sync.dma_start(out=raw[:], in_=xa[pair * PAIR:(pair + 1) * PAIR, :].rearrange("(i p) k -> p i k", p=PART))
+            for i in range(2):
+                made["x_rows", A, 2 * pair + i] = raw[:, i, :]
+
+        def load_xb(pair):
+            raw = keep.tile([PART, 2, P], U8, name="xb_fp8_%d" % pair)
+            nc.sync.dma_start(out=raw[:], in_=xb_bytes[pair * PAIR:(pair + 1) * PAIR, :].rearrange("(i p) k -> p i k", p=PART))
+            made["xb_fp8", pair] = raw
 
         def spread_scale():
-            for half in range(P // BANK):
-                bank = new_bank([PART, PACK, PART])
-                for i in range(PACK):
-                    col = half * PACK + i
+            for b in range(P // BANK):
+                bank = new_bank([PART, SLOTS, PART])
+                for i in range(SLOTS):
+                    col = b * SLOTS + i
                     nc.tensor.transpose(bank[:, i, :], scale_cols[:, col:col + 1].to_broadcast([PART, PART]), ident[:])
-                nc.scalar.activation(out=scale_spread[:, half * BANK:(half + 1) * BANK].rearrange("p (m i) -> p m i", i=PACK),
+                nc.scalar.activation(out=scale_spread[:, b * BANK:(b + 1) * BANK].rearrange("p (m i) -> p m i", i=SLOTS),
                                      in_=bank[:].rearrange("p i m -> p m i"), func=COPY)
 
         def turn_factors():
             bank = new_bank([PART, PASSES, PART], dtype=BF16)
             for h in range(PASSES):
                 nc.tensor.transpose(bank[:, h, :], factor_rows[:, h * PART:(h + 1) * PART], ident_bf16[:])
-            nc.scalar.activation(out=ca_cols[:], in_=bank[:, :, 0:PACK], func=COPY, scale=-1.0 / P)
-            nc.scalar.copy(out=cb_cols[:], in_=bank[:, :, PACK:2 * PACK])
-
-        def group_v(g, h, on_scalar):
-            grouped = work.tile([PART, PACK, PART * PACK], BF16, name="v_grouped", align_bytes=64, bufs=2)
-            cut = PACK - on_scalar
-            for slots, copy in ((slice(0, cut), nc.vector.tensor_copy), (slice(cut, PACK), nc.scalar.copy)):
-                if slots.start < slots.stop:
-                    copy(out=grouped[:, slots, :].rearrange("p t (q r j) -> p t q j r", r=8, j=PACK),
-                         in_=t["v_raw", g, h][:].rearrange("p j (q t r) -> p t q j r", t=PACK, r=8)[:, slots])
-            t["v_grouped", g, h] = grouped[:].rearrange("p t c -> p (t c)")
-
-        def quantize(name, key, grouped):
-            width = grouped.shape[1] // PACK
-            tag = name + "".join("_%d" % i for i in key)
-            codes = keep.tile([PART, width], U32, name=tag + "_codes", align_bytes=64)
-            scales = keep.tile([PART, width], U8, name=tag + "_scales", align_bytes=64)
-            nc.vector.quantize_mx(out=codes[:].bitcast(FP8X4), scales=scales[:], in_=grouped)
-            t[(name,) + key] = (codes, scales)
-
-        def quantize_v(g, h):
-            quantize("vq", (g, h), t["v_grouped", g, h])
-
-        def mx(acc, stationary, s_cols, moving, m_cols, start, stop):
-            nc.tensor.matmul_mx(
-                out=acc, lhsT=stationary[0][:, s_cols].bitcast(FP8X4), lhsT_scale=stationary[1][:, s_cols],
-                rhs=moving[0][:, m_cols].bitcast(FP8X4), rhs_scale=moving[1][:, m_cols], start=start, stop=stop)
-
-        def widen_xb(j):
-            rows = work.tile([PART, P], BF16, name="xb_rows", bufs=4)
-            nc.vector.tensor_tensor(out=rows[:], in0=t["xb_fp8", j // 2][:, j % 2, :].bitcast(FP8), in1=scale_spread[:], op=ALU.mult)
-            t["x_rows", 1, j] = rows[:]
-
-        def turn_x(run, m, g):
-            half, pair = divmod(m, 2)
-            if pair == 0:
-                t["x_grouped", run, half, g] = work.tile([PART, HALF * PACK], BF16, name="x_grouped", align_bytes=64, bufs=4)
-            bank = new_bank([PART, 2, PAIR])
-            for i in range(2):
-                words = t["x_rows", run, 2 * m + i].bitcast(F32)
-                for u in range(2):
-                    nc.tensor.transpose(bank[:, u, i * PART:(i + 1) * PART],
-                                        words[:, 256 * g + u:256 * (g + 1):2], ident[:])
-            cols = slice(pair * PAIR * PACK, (pair + 1) * PAIR * PACK)
-            nc.scalar.copy(out=t["x_grouped", run, half, g][:, cols].bitcast(F32).rearrange("p (c u) -> p c u", u=2),
-                           in_=bank[:].rearrange("p u c -> p c u"))
-
-        def quantize_x(run, half, g):
-            quantize("xq", (run, half, g), t["x_grouped", run, half, g][:])
-
-        def whiten(run, half, h):
-            white = work.tile([PART, PACK, HALF], F32, name="white", bufs=6)
-            for s in range(PACK):
-                bank = new_bank([PART, HALF])
-                for g in range(PASSES):
-                    mx(bank[:], t["vq", g, h], slice(s * PART, (s + 1) * PART), t["xq", run, half, g], slice(0, HALF),
-                       g == 0, g == PASSES - 1)
-                nc.scalar.activation(out=white[:, s, :], in_=bank[:], func=COPY, scale=(ca_cols, cb_cols)[run][:, h, s:s + 1])
-            t["white", run, half, h] = white
-
-        def white_cols(run, n, h):
-            half, c0 = divmod(FIRST[n] * PART, HALF)
-            return t["white", run, half, h][:, :, c0:c0 + TILES[n] * PART]
-
-        def group_ab(run, n, h, copy):
-            grouped = work.tile([PART, TILES[n] * PART, PACK], BF16, name="ab_grouped", align_bytes=64, bufs=4)
-            copy(out=grouped[:].rearrange("p (c i) s -> p c s i", i=4),
-                 in_=white_cols(run, n, h).rearrange("p s (c i) -> p c s i", i=4))
-            t["ab_grouped", run, n, h] = grouped
-
-        abq = {}
-        for run in range(2):
-            for h in range(PASSES):
-                ab_codes = keep.tile([PART, C], U32, name="ab_codes_%d_%d" % (run, h), align_bytes=64)
-                ab_scales = keep.tile([PART, C], U8, name="ab_scales_%d_%d" % (run, h), align_bytes=64)
-                abq[run, h] = (ab_codes, ab_scales)
-
-        def quantize_ab(run, n, h):
-            cols = slice(FIRST[n] * PART, FIRST[n + 1] * PART)
-            codes, scales = abq[run, h]
-            nc.vector.quantize_mx(out=codes[:, cols].bitcast(FP8X4), scales=scales[:, cols],
-                                  in_=t["ab_grouped", run, n, h][:].rearrange("p c s -> p (c s)"))
-
-        def products(n, h):
-            prod = work.tile([PART, PACK, TILES[n] * PART], F32, name="prod", bufs=4)
-            nc.vector.tensor_tensor(out=prod[:], in0=white_cols(0, n, h), in1=white_cols(1, n, h), op=ALU.mult)
-            t["prod", n, h] = prod
-
-        def sum_products(n):
-            bank = new_bank([PART, TILES[n], PART])
-            for i in range(TILES[n]):
-                for h in range(PASSES):
-                    for s in range(PACK):
-                        nc.tensor.matmul(bank[:, i, :], lhsT=t["prod", n, h][:, s, i * PART:(i + 1) * PART], rhs=ident[:],
-                                         is_transpose=True, start=(h == 0 and s == 0), stop=(h == PASSES - 1 and s == PACK - 1))
-            t["e_bank", n] = bank
-
-        def reduce_e(n):
-            nc.vector.tensor_reduce(out=e_cols[:, FIRST[n]:FIRST[n + 1]], in_=t["e_bank", n][:], axis=mybir.AxisListType.X, op=ALU.add)
-
-        def spread_e(n):
-            bank = new_bank([PART, TILES[n], PART])
-            for i in range(TILES[n]):
-                col = FIRST[n] + i
-                nc.tensor.transpose(bank[:, i, :], e_cols[:, col:col + 1].to_broadcast([PART, PART]), ident[:])
-            nc.scalar.copy(out=e_spread[:, FIRST[n] * PART:FIRST[n + 1] * PART], in_=bank[:].rearrange("p i m -> p (i m)"))
-
-        e_spread = keep.tile([PART, C], F32, name="e_spread")
-
-        def gram(row, b):
-            c0, c1 = b * BANK, min((b + 1) * BANK, (row // 2 + 1) * PAIR)
-            bank = new_bank([PART, c1 - c0])
-            p0 = c0
-            for n_cols in (512, 256, 128):
-                if p0 + n_cols <= c1:
-                    for h in range(PASSES):
-                        for run in range(2):
-                            mx(bank[:, p0 - c0:p0 - c0 + n_cols], abq[run, h], slice(row * PART, (row + 1) * PART),
-                               abq[1 - run, h], slice(p0, p0 + n_cols), h == 0 and run == 0, h == PASSES - 1 and run == 1)
-                    p0 = p0 + n_cols
-            t["gram", row, b] = bank
-
-        def finish(row, b):
-            cols = slice(b * BANK, min((b + 1) * BANK, (row // 2 + 1) * PAIR))
-            rows = keep.tile([PART, cols.stop - cols.start], F32, name="rows_%d_%d" % (row, b))
-            nc.vector.scalar_tensor_tensor(out=rows[:], in0=t["gram", row, b][:], scalar=e_cols[:, row:row + 1],
-                                           in1=e_spread[:, cols], op0=ALU.subtract, op1=ALU.subtract)
-            nc.sync.dma_start(out=out[row * PART:(row + 1) * PART, cols], in_=rows[:])
-            t["rows", row, b] = rows
-
-        def mirror(rows, cols):
-            bank = new_bank([PART, len(cols), len(rows) * PART])
-            for j, col in enumerate(cols):
-                b, c0 = divmod(col * PART, BANK)
-                for i, row in enumerate(rows):
-                    nc.tensor.transpose(bank[:, j, i * PART:(i + 1) * PART], t["rows", row, b][:, c0:c0 + PART], ident[:])
-            mirrored = keep.tile([PART, len(cols), len(rows) * PART], F32, name="mirrored_%d_%d" % (rows[0], cols[0]))
-            nc.scalar.copy(out=mirrored[:], in_=bank[:])
-            target = out[cols[0] * PART:(cols[-1] + 1) * PART, rows[0] * PART:(rows[-1] + 1) * PART]
-            nc.sync.dma_start(out=target.rearrange("(j p) c -> p j c", p=PART), in_=mirrored[:])
+            nc.scalar.activation(out=ca_cols[:], in_=bank[:, :, 0:SLOTS], func=COPY, scale=-1.0 / P)
+            nc.scalar.copy(out=cb_cols[:], in_=bank[:, :, SLOTS:2 * SLOTS])
 
         def warm(count):
             bank = new_bank([PART, BANK])
             for i in range(count):
                 nc.tensor.matmul(bank[:], lhsT=warm_in[:, 0:PART], rhs=warm_in[:], start=True, stop=True)
 
-        on_v, on_s = nc.vector.tensor_copy, nc.scalar.copy
+        def quantize(name, grouped):
+            width = grouped.shape[1] // SLOTS
+            codes = keep.tile([PART, width], U32, name=name + "_codes", align_bytes=64)
+            scales = keep.tile([PART, width], U8, name=name + "_scales", align_bytes=64)
+            nc.vector.quantize_mx(out=codes[:].bitcast(FP8X4), scales=scales[:], in_=grouped)
+            return codes, scales
+
+        def mx(acc, stationary, s_cols, moving, m_cols, start, stop):
+            nc.tensor.matmul_mx(
+                out=acc, lhsT=stationary[0][:, s_cols].bitcast(FP8X4), lhsT_scale=stationary[1][:, s_cols],
+                rhs=moving[0][:, m_cols].bitcast(FP8X4), rhs_scale=moving[1][:, m_cols], start=start, stop=stop)
+
+        def group_v(g, h, scalar_slots):
+            grouped = work.tile([PART, SLOTS, PART * SLOTS], BF16, name="v_grouped", align_bytes=64)
+            cut = SLOTS - scalar_slots
+            source = made["v_raw", g, h][:].rearrange("p j (q s r) -> p s q j r", s=SLOTS, r=RUN_LEN)
+            target = grouped[:].rearrange("p s (q r j) -> p s q j r", r=RUN_LEN, j=SLOTS)
+            on_vector(out=target[:, 0:cut], in_=source[:, 0:cut])
+            if scalar_slots:
+                on_scalar(out=target[:, cut:SLOTS], in_=source[:, cut:SLOTS])
+            made["v_grouped", g, h] = grouped
+
+        def quantize_v(g, h):
+            made["v_q", g, h] = quantize("v_q_%d_%d" % (g, h), made["v_grouped", g, h][:].rearrange("p s c -> p (s c)"))
+
+        def widen_xb(tile):
+            rows = work.tile([PART, P], BF16, name="xb_rows", bufs=4)
+            nc.vector.tensor_tensor(out=rows[:], in0=made["xb_fp8", tile // 2][:, tile % 2, :].bitcast(FP8),
+                                    in1=scale_spread[:], op=ALU.mult)
+            made["x_rows", B, tile] = rows[:]
+
+        def turn_x(run, pair):
+            half, second = divmod(pair, 2)
+            words_a_pass = K_PASS // 2
+            for g in range(PASSES):
+                if not second:
+                    made["x_grouped", run, half, g] = work.tile([PART, HALF * SLOTS], BF16, name="x_grouped", align_bytes=64, bufs=4)
+                bank = new_bank([PART, 2, PAIR])
+                for i in range(2):
+                    words = made["x_rows", run, 2 * pair + i].bitcast(F32)
+                    for u in range(2):
+                        nc.tensor.transpose(bank[:, u, i * PART:(i + 1) * PART],
+                                            words[:, words_a_pass * g + u:words_a_pass * (g + 1):2], ident[:])
+                cols = slice(second * PAIR * SLOTS, (second + 1) * PAIR * SLOTS)
+                nc.scalar.copy(out=made["x_grouped", run, half, g][:, cols].bitcast(F32).rearrange("p (c u) -> p c u", u=2),
+                               in_=bank[:].rearrange("p u c -> p c u"))
+
+        def quantize_x(run, half, g):
+            made["x_q", run, half, g] = quantize("x_q_%d_%d_%d" % (run, half, g), made["x_grouped", run, half, g][:])
+
+        def whiten(run, half, h):
+            white = work.tile([PART, SLOTS, HALF], F32, name="white", bufs=6)
+            for s in range(SLOTS):
+                bank = new_bank([PART, HALF])
+                for g in range(PASSES):
+                    mx(bank[:], made["v_q", g, h], slice(s * PART, (s + 1) * PART), made["x_q", run, half, g], slice(0, HALF),
+                       g == 0, g == PASSES - 1)
+                nc.scalar.activation(out=white[:, s, :], in_=bank[:], func=COPY, scale=(ca_cols, cb_cols)[run][:, h, s:s + 1])
+            made["white", run, half, h] = white
+
+        def white_cols(run, pair, h):
+            half, second = divmod(pair, 2)
+            return made["white", run, half, h][:, :, second * PAIR:(second + 1) * PAIR]
+
+        def group_white(run, pair, h, copy):
+            grouped = work.tile([PART, PAIR, SLOTS], BF16, name="white_grouped", align_bytes=64, bufs=4)
+            copy(out=grouped[:].rearrange("p (c i) s -> p c s i", i=LINE),
+                 in_=white_cols(run, pair, h).rearrange("p s (c i) -> p c s i", i=LINE))
+            made["white_grouped", run, pair, h] = grouped
+
+        def quantize_white(run, pair, h):
+            cols = slice(pair * PAIR, (pair + 1) * PAIR)
+            codes, scales = white_q[run, h]
+            nc.vector.quantize_mx(out=codes[:, cols].bitcast(FP8X4), scales=scales[:, cols],
+                                  in_=made["white_grouped", run, pair, h][:].rearrange("p c s -> p (c s)"))
+
+        def products(pair, h):
+            prod = work.tile([PART, SLOTS, PAIR], F32, name="prod", bufs=4)
+            nc.vector.tensor_tensor(out=prod[:], in0=white_cols(A, pair, h), in1=white_cols(B, pair, h), op=ALU.mult)
+            made["prod", pair, h] = prod
+
+        def sum_products(pair):
+            bank = new_bank([PART, 2, PART])
+            for i in range(2):
+                for h in range(PASSES):
+                    for s in range(SLOTS):
+                        nc.tensor.matmul(bank[:, i, :], lhsT=made["prod", pair, h][:, s, i * PART:(i + 1) * PART], rhs=ident[:],
+                                         is_transpose=True, start=(h == 0 and s == 0), stop=(h == PASSES - 1 and s == SLOTS - 1))
+            made["e_bank", pair] = bank
+
+        def reduce_e(pair):
+            nc.vector.tensor_reduce(out=e_cols[:, 2 * pair:2 * pair + 2], in_=made["e_bank", pair][:],
+                                    axis=mybir.AxisListType.X, op=ALU.add)
+
+        def spread_e(pair):
+            bank = new_bank([PART, 2, PART])
+            for i in range(2):
+                col = 2 * pair + i
+                nc.tensor.transpose(bank[:, i, :], e_cols[:, col:col + 1].to_broadcast([PART, PART]), ident[:])
+            nc.scalar.copy(out=e_spread[:, pair * PAIR:(pair + 1) * PAIR], in_=bank[:].rearrange("p i m -> p (i m)"))
+
+        def out_cols(tile, half):
+            return slice(half * HALF, min((half + 1) * HALF, (tile // 2 + 1) * PAIR))
+
+        def gram(tile, half):
+            cols = out_cols(tile, half)
+            bank = new_bank([PART, cols.stop - cols.start])
+            for h in range(PASSES):
+                for run in (A, B):
+                    mx(bank[:], white_q[run, h], slice(tile * PART, (tile + 1) * PART), white_q[1 - run, h], cols,
+                       h == 0 and run == A, h == PASSES - 1 and run == B)
+            made["gram", tile, half] = bank
+
+        def finish(tile, half):
+            cols = out_cols(tile, half)
+            rows = keep.tile([PART, cols.stop - cols.start], F32, name="rows_%d_%d" % (tile, half))
+            nc.vector.scalar_tensor_tensor(out=rows[:], in0=made["gram", tile, half][:], scalar=e_cols[:, tile:tile + 1],
+                                           in1=e_spread[:, cols], op0=ALU.subtract, op1=ALU.subtract)
+            nc.sync.dma_start(out=out[tile * PART:(tile + 1) * PART, cols], in_=rows[:])
+            made["rows", tile, half] = rows
+
+        def mirror(pair, earlier):
+            half, second = divmod(earlier, 2)
+            bank = new_bank([PART, 2, PAIR])
+            for j in range(2):
+                c0 = second * PAIR + j * PART
+                for i in range(2):
+                    nc.tensor.transpose(bank[:, j, i * PART:(i + 1) * PART],
+                                        made["rows", 2 * pair + i, half][:, c0:c0 + PART], ident[:])
+            mirrored = keep.tile([PART, 2, PAIR], F32, name="mirrored_%d_%d" % (pair, earlier))
+            nc.scalar.copy(out=mirrored[:], in_=bank[:])
+            target = out[earlier * PAIR:(earlier + 1) * PAIR, pair * PAIR:(pair + 1) * PAIR]
+            nc.sync.dma_start(out=target.rearrange("(j p) c -> p j c", p=PART), in_=mirrored[:])
+
         load_scale()
         load_v(0, 0)
         load_xb(0)
@@ -260,137 +266,126 @@ def tile_crossnobisdissimilaritymatrix_kernel(tc, xa, xb_bytes, xb_scale, v, ca,
         load_xa(3)
         load_xb(3)
         load_v(1, 1)
-        warm(4)
+
+        warm(WARM_FIRST)
         spread_scale()
-        warm(7)
-        group_v(0, 0, 2)
+        warm(WARM_SECOND)
+        group_v(0, 0, V_SLOTS_ON_SCALAR[0])
         turn_factors()
-        turn_x(0, 0, 0)
-        turn_x(0, 0, 1)
+        turn_x(A, 0)
         widen_xb(0)
         widen_xb(1)
-        turn_x(1, 0, 0)
-        turn_x(1, 0, 1)
+        turn_x(B, 0)
         widen_xb(2)
         widen_xb(3)
-        group_v(1, 0, 1)
-        warm(3)
-        turn_x(0, 1, 0)
-        turn_x(0, 1, 1)
-        turn_x(1, 1, 0)
-        turn_x(1, 1, 1)
-        warm(2)
-        quantize_v(0, 0)
-        quantize_x(0, 0, 0)
-        quantize_v(1, 0)
-        quantize_x(0, 0, 1)
-        turn_x(0, 2, 0)
-        turn_x(0, 2, 1)
-        whiten(0, 0, 0)
-        quantize_x(1, 0, 0)
-        quantize_x(1, 0, 1)
-        group_v(0, 1, 0)
-        whiten(1, 0, 0)
-        group_v(1, 1, 0)
-        quantize_v(0, 1)
-        quantize_v(1, 1)
-        turn_x(0, 3, 0)
-        turn_x(0, 3, 1)
-        whiten(0, 0, 1)
+        group_v(1, 0, V_SLOTS_ON_SCALAR[1])
+        warm(WARM_BETWEEN)
+        turn_x(A, 1)
+        turn_x(B, 1)
+        warm(WARM_BETWEEN)
+        for g in range(PASSES):
+            quantize_v(g, 0)
+            quantize_x(A, 0, g)
+        turn_x(A, 2)
+
+        whiten(A, 0, 0)
+        for g in range(PASSES):
+            quantize_x(B, 0, g)
+        whiten(B, 0, 0)
+        for g in range(PASSES):
+            group_v(g, 1, 0)
+        for g in range(PASSES):
+            quantize_v(g, 1)
+        whiten(A, 0, 1)
         widen_xb(4)
         widen_xb(5)
-        turn_x(1, 2, 0)
-        turn_x(1, 2, 1)
+        turn_x(A, 3)
+        turn_x(B, 2)
         widen_xb(6)
         widen_xb(7)
-        whiten(1, 0, 1)
-        quantize_x(0, 1, 0)
-        quantize_x(0, 1, 1)
-        turn_x(1, 3, 0)
-        turn_x(1, 3, 1)
-        products(0, 0)
-        products(1, 0)
-        whiten(0, 1, 0)
-        group_ab(0, 0, 0, on_v)
-        quantize_x(1, 1, 0)
-        quantize_x(1, 1, 1)
-        group_ab(0, 1, 0, on_v)
-        whiten(1, 1, 0)
-        products(0, 1)
-        products(1, 1)
-        group_ab(1, 0, 0, on_v)
-        group_ab(1, 1, 0, on_v)
-        for run in (0, 1):
-            for n in (0, 1):
-                quantize_ab(run, n, 0)
-        whiten(0, 1, 1)
-        sum_products(0)
-        group_ab(1, 0, 1, on_v)
-        group_ab(1, 1, 1, on_v)
-        group_ab(0, 0, 1, on_v)
-        group_ab(0, 1, 1, on_s)
-        whiten(1, 1, 1)
-        sum_products(1)
-        for run in (1, 0):
-            for n in (0, 1):
-                quantize_ab(run, n, 1)
-        reduce_e(0)
+        whiten(B, 0, 1)
+        for g in range(PASSES):
+            quantize_x(A, 1, g)
+        turn_x(B, 3)
+
+        for pair in (0, 1):
+            products(pair, 0)
+        whiten(A, 1, 0)
+        for pair in (0, 1):
+            group_white(A, pair, 0, on_vector)
+        for g in range(PASSES):
+            quantize_x(B, 1, g)
+        whiten(B, 1, 0)
+        for pair in (0, 1):
+            products(pair, 1)
+        for pair in (0, 1):
+            group_white(B, pair, 0, on_vector)
+        for run in (A, B):
+            for pair in (0, 1):
+                quantize_white(run, pair, 0)
+        whiten(A, 1, 1)
+        for run in (B, A):
+            for pair in (0, 1):
+                group_white(run, pair, 1, on_vector)
+        whiten(B, 1, 1)
+        for pair in (0, 1):
+            sum_products(pair)
+        for run in (B, A):
+            for pair in (0, 1):
+                quantize_white(run, pair, 1)
+
         products(2, 0)
-        group_ab(0, 2, 0, on_v)
-        group_ab(1, 2, 0, on_s)
-        group_ab(0, 2, 1, on_s)
-        group_ab(1, 2, 1, on_s)
+        reduce_e(0)
+        for h in range(PASSES):
+            for run in (A, B):
+                group_white(run, 2, h, on_scalar)
         gram(3, 0)
         gram(2, 0)
         reduce_e(1)
         products(2, 1)
-        quantize_ab(0, 2, 0)
-        quantize_ab(1, 2, 0)
+        for run in (A, B):
+            quantize_white(run, 2, 0)
         spread_e(0)
         spread_e(1)
         products(3, 0)
-        quantize_ab(0, 2, 1)
-        quantize_ab(1, 2, 1)
+        for run in (A, B):
+            quantize_white(run, 2, 1)
         sum_products(2)
-        group_ab(0, 3, 0, on_s)
-        group_ab(1, 3, 0, on_s)
-        finish(3, 0)
-        finish(2, 0)
+
+        for run in (A, B):
+            group_white(run, 3, 0, on_scalar)
+        products(3, 1)
         gram(5, 0)
         reduce_e(2)
+        finish(3, 0)
+        finish(2, 0)
         gram(4, 0)
-        group_ab(0, 3, 1, on_s)
-        group_ab(1, 3, 1, on_s)
-        products(3, 1)
-        quantize_ab(0, 3, 0)
-        finish(5, 0)
+        group_white(A, 3, 1, on_scalar)
+        group_white(B, 3, 1, on_vector)
         sum_products(3)
-        quantize_ab(1, 3, 0)
-        finish(4, 0)
-        quantize_ab(0, 3, 1)
+        for run in (A, B):
+            quantize_white(run, 3, 0)
+        quantize_white(B, 3, 1)
         reduce_e(3)
-        quantize_ab(1, 3, 1)
-        mirror((2, 3), (0, 1))
+        quantize_white(A, 3, 1)
+        mirror(1, 0)
         spread_e(2)
-        mirror((4, 5), (0, 1))
-        mirror((4, 5), (2, 3))
-        spread_e(3)
-        gram(7, 0)
-        gram(6, 0)
-        finish(7, 0)
-        gram(7, 1)
-        finish(6, 0)
-        gram(6, 1)
-        finish(7, 1)
-        mirror((6, 7), (0, 1))
-        mirror((6, 7), (2, 3))
-        finish(6, 1)
-        gram(5, 1)
-        mirror((6, 7), (4, 5))
-        gram(4, 1)
-        finish(5, 1)
         gram(1, 0)
-        finish(4, 1)
+        for tile in (5, 4, 1):
+            finish(tile, 0)
+
+        for tile in (7, 6):
+            gram(tile, 0)
+        for tile in (7, 6):
+            finish(tile, 0)
+        spread_e(3)
+        for pair in (2, 3):
+            for earlier in (0, 1):
+                mirror(pair, earlier)
+        for tile in (7, 6, 5, 4):
+            gram(tile, 1)
+        for tile in (7, 6, 5, 4):
+            finish(tile, 1)
+        mirror(3, 2)
         gram(0, 0)
-        finish(1, 0)
         finish(0, 0)

@@ -88,13 +88,13 @@ def tile_crossnobisdissimilaritymatrix_kernel(tc, xa, xb_bytes, xb_scale, v, ca,
 
         def load_xa(pair):
             raw = keep.tile([PART, 2, P], BF16, name="xa_raw_%d" % pair)
-            nc.sync.dma_start(out=raw[:], in_=xa[pair * PAIR:(pair + 1) * PAIR, :].rearrange("(i p) k -> p i k", p=PART))
+            nc.sync.dma_start(out=raw[:], in_=xa[pair * PAIR:(pair + 1) * PAIR, :].rearrange("(p i) k -> p i k", i=2))
             for i in range(2):
-                made["x_rows", A, 2 * pair + i] = raw[:, i, :]
+                made["x_rows", A, pair, i] = raw[:, i, :]
 
         def load_xb(pair):
             raw = keep.tile([PART, 2, P], U8, name="xb_fp8_%d" % pair)
-            nc.sync.dma_start(out=raw[:], in_=xb_bytes[pair * PAIR:(pair + 1) * PAIR, :].rearrange("(i p) k -> p i k", p=PART))
+            nc.sync.dma_start(out=raw[:], in_=xb_bytes[pair * PAIR:(pair + 1) * PAIR, :].rearrange("(p i) k -> p i k", i=2))
             made["xb_fp8", pair] = raw
 
         def spread_scale():
@@ -120,8 +120,8 @@ def tile_crossnobisdissimilaritymatrix_kernel(tc, xa, xb_bytes, xb_scale, v, ca,
 
         def quantize(name, grouped):
             width = grouped.shape[1] // SLOTS
-            codes = keep.tile([PART, width], U32, name=name + "_codes", align_bytes=64)
-            scales = keep.tile([PART, width], U8, name=name + "_scales", align_bytes=64)
+            codes = work.tile([PART, width], U32, name=name + "_codes", align_bytes=64, bufs=4)
+            scales = work.tile([PART, width], U8, name=name + "_scales", align_bytes=64, bufs=4)
             nc.vector.quantize_mx(out=codes[:].bitcast(FP8X4), scales=scales[:], in_=grouped)
             return codes, scales
 
@@ -141,13 +141,14 @@ def tile_crossnobisdissimilaritymatrix_kernel(tc, xa, xb_bytes, xb_scale, v, ca,
             made["v_grouped", g, h] = grouped
 
         def quantize_v(g, h):
-            made["v_q", g, h] = quantize("v_q_%d_%d" % (g, h), made["v_grouped", g, h][:].rearrange("p s c -> p (s c)"))
+            made["v_q", g, h] = quantize("v", made["v_grouped", g, h][:].rearrange("p s c -> p (s c)"))
 
-        def widen_xb(tile):
-            rows = work.tile([PART, P], BF16, name="xb_rows", bufs=4)
-            nc.vector.tensor_tensor(out=rows[:], in0=made["xb_fp8", tile // 2][:, tile % 2, :].bitcast(FP8),
-                                    in1=scale_spread[:], op=ALU.mult)
-            made["x_rows", B, tile] = rows[:]
+        def widen_xb(pair):
+            for i in range(2):
+                rows = work.tile([PART, P], BF16, name="xb_rows", bufs=4)
+                nc.vector.tensor_tensor(out=rows[:], in0=made["xb_fp8", pair][:, i, :].bitcast(FP8),
+                                        in1=scale_spread[:], op=ALU.mult)
+                made["x_rows", B, pair, i] = rows[:]
 
         def turn_x(run, pair):
             half, second = divmod(pair, 2)
@@ -157,16 +158,16 @@ def tile_crossnobisdissimilaritymatrix_kernel(tc, xa, xb_bytes, xb_scale, v, ca,
                     made["x_grouped", run, half, g] = work.tile([PART, HALF * SLOTS], BF16, name="x_grouped", align_bytes=64, bufs=4)
                 bank = new_bank([PART, 2, PAIR])
                 for i in range(2):
-                    words = made["x_rows", run, 2 * pair + i].bitcast(F32)
+                    words = made["x_rows", run, pair, i].bitcast(F32)
                     for u in range(2):
                         nc.tensor.transpose(bank[:, u, i * PART:(i + 1) * PART],
                                             words[:, words_a_pass * g + u:words_a_pass * (g + 1):2], ident[:])
                 cols = slice(second * PAIR * SLOTS, (second + 1) * PAIR * SLOTS)
-                nc.scalar.copy(out=made["x_grouped", run, half, g][:, cols].bitcast(F32).rearrange("p (c u) -> p c u", u=2),
-                               in_=bank[:].rearrange("p u c -> p c u"))
+                nc.scalar.copy(out=made["x_grouped", run, half, g][:, cols].bitcast(F32).rearrange("p (m i u) -> p m i u", i=2, u=2),
+                               in_=bank[:].rearrange("p u (i m) -> p m i u", i=2))
 
         def quantize_x(run, half, g):
-            made["x_q", run, half, g] = quantize("x_q_%d_%d_%d" % (run, half, g), made["x_grouped", run, half, g][:])
+            made["x_q", run, half, g] = quantize("x", made["x_grouped", run, half, g][:])
 
         def whiten(run, half, h):
             white = work.tile([PART, SLOTS, HALF], F32, name="white", bufs=6)
@@ -178,26 +179,27 @@ def tile_crossnobisdissimilaritymatrix_kernel(tc, xa, xb_bytes, xb_scale, v, ca,
                 nc.scalar.activation(out=white[:, s, :], in_=bank[:], func=COPY, scale=(ca_cols, cb_cols)[run][:, h, s:s + 1])
             made["white", run, half, h] = white
 
-        def white_cols(run, pair, h):
-            half, second = divmod(pair, 2)
-            return made["white", run, half, h][:, :, second * PAIR:(second + 1) * PAIR]
+        def white_cols(run, pairs, h):
+            half, second = divmod(pairs[0], 2)
+            return made["white", run, half, h][:, :, second * PAIR:(second + len(pairs)) * PAIR]
 
-        def group_white(run, pair, h, copy):
-            grouped = work.tile([PART, PAIR, SLOTS], BF16, name="white_grouped", align_bytes=64, bufs=4)
+        def group_white(run, pairs, h, copy):
+            grouped = work.tile([PART, len(pairs) * PAIR, SLOTS], BF16, name="white_grouped", align_bytes=64, bufs=3)
             copy(out=grouped[:].rearrange("p (c i) s -> p c s i", i=LINE),
-                 in_=white_cols(run, pair, h).rearrange("p s (c i) -> p c s i", i=LINE))
-            made["white_grouped", run, pair, h] = grouped
+                 in_=white_cols(run, pairs, h).rearrange("p s (c i) -> p c s i", i=LINE))
+            made["white_grouped", run, pairs, h] = grouped
 
-        def quantize_white(run, pair, h):
-            cols = slice(pair * PAIR, (pair + 1) * PAIR)
+        def quantize_white(run, pairs, h):
+            cols = slice(pairs[0] * PAIR, (pairs[-1] + 1) * PAIR)
             codes, scales = white_q[run, h]
             nc.vector.quantize_mx(out=codes[:, cols].bitcast(FP8X4), scales=scales[:, cols],
-                                  in_=made["white_grouped", run, pair, h][:].rearrange("p c s -> p (c s)"))
+                                  in_=made["white_grouped", run, pairs, h][:].rearrange("p c s -> p (c s)"))
 
-        def products(pair, h):
-            prod = work.tile([PART, SLOTS, PAIR], F32, name="prod", bufs=4)
-            nc.vector.tensor_tensor(out=prod[:], in0=white_cols(A, pair, h), in1=white_cols(B, pair, h), op=ALU.mult)
-            made["prod", pair, h] = prod
+        def products(pairs, h):
+            prod = work.tile([PART, SLOTS, len(pairs) * PAIR], F32, name="prod", bufs=3)
+            nc.vector.tensor_tensor(out=prod[:], in0=white_cols(A, pairs, h), in1=white_cols(B, pairs, h), op=ALU.mult)
+            for n, pair in enumerate(pairs):
+                made["prod", pair, h] = prod[:, :, n * PAIR:(n + 1) * PAIR]
 
         def sum_products(pair):
             bank = new_bank([PART, 2, PART])
@@ -247,7 +249,7 @@ def tile_crossnobisdissimilaritymatrix_kernel(tc, xa, xb_bytes, xb_scale, v, ca,
                 for i in range(2):
                     nc.tensor.transpose(bank[:, j, i * PART:(i + 1) * PART],
                                         made["rows", 2 * pair + i, half][:, c0:c0 + PART], ident[:])
-            mirrored = keep.tile([PART, 2, PAIR], F32, name="mirrored_%d_%d" % (pair, earlier))
+            mirrored = work.tile([PART, 2, PAIR], F32, name="mirrored", bufs=5)
             nc.scalar.copy(out=mirrored[:], in_=bank[:])
             target = out[earlier * PAIR:(earlier + 1) * PAIR, pair * PAIR:(pair + 1) * PAIR]
             nc.sync.dma_start(out=target.rearrange("(j p) c -> p j c", p=PART), in_=mirrored[:])
@@ -274,10 +276,8 @@ def tile_crossnobisdissimilaritymatrix_kernel(tc, xa, xb_bytes, xb_scale, v, ca,
         turn_factors()
         turn_x(A, 0)
         widen_xb(0)
-        widen_xb(1)
         turn_x(B, 0)
-        widen_xb(2)
-        widen_xb(3)
+        widen_xb(1)
         group_v(1, 0, V_SLOTS_ON_SCALAR[1])
         warm(WARM_BETWEEN)
         turn_x(A, 1)
@@ -297,77 +297,70 @@ def tile_crossnobisdissimilaritymatrix_kernel(tc, xa, xb_bytes, xb_scale, v, ca,
         for g in range(PASSES):
             quantize_v(g, 1)
         whiten(A, 0, 1)
-        widen_xb(4)
-        widen_xb(5)
+        widen_xb(2)
         turn_x(A, 3)
         turn_x(B, 2)
-        widen_xb(6)
-        widen_xb(7)
+        widen_xb(3)
         whiten(B, 0, 1)
         for g in range(PASSES):
             quantize_x(A, 1, g)
         turn_x(B, 3)
 
-        for pair in (0, 1):
-            products(pair, 0)
+        first_half = (0, 1)
+        products(first_half, 0)
         whiten(A, 1, 0)
-        for pair in (0, 1):
-            group_white(A, pair, 0, on_vector)
+        group_white(A, first_half, 0, on_vector)
         for g in range(PASSES):
             quantize_x(B, 1, g)
         whiten(B, 1, 0)
-        for pair in (0, 1):
-            products(pair, 1)
-        for pair in (0, 1):
-            group_white(B, pair, 0, on_vector)
-        for run in (A, B):
-            for pair in (0, 1):
-                quantize_white(run, pair, 0)
+        group_white(B, first_half, 0, on_vector)
+        products(first_half, 1)
         whiten(A, 1, 1)
+        for run in (A, B):
+            quantize_white(run, first_half, 0)
         for run in (B, A):
-            for pair in (0, 1):
-                group_white(run, pair, 1, on_vector)
+            group_white(run, first_half, 1, on_vector)
         whiten(B, 1, 1)
-        for pair in (0, 1):
+        for pair in first_half:
             sum_products(pair)
+        products((2,), 0)
         for run in (B, A):
-            for pair in (0, 1):
-                quantize_white(run, pair, 1)
+            quantize_white(run, first_half, 1)
 
-        products(2, 0)
         reduce_e(0)
-        for h in range(PASSES):
-            for run in (A, B):
-                group_white(run, 2, h, on_scalar)
+        for run in (A, B):
+            group_white(run, (2,), 0, on_scalar)
         gram(3, 0)
         gram(2, 0)
         reduce_e(1)
-        products(2, 1)
+        products((2,), 1)
         for run in (A, B):
-            quantize_white(run, 2, 0)
+            quantize_white(run, (2,), 0)
+        for run in (A, B):
+            group_white(run, (2,), 1, on_scalar)
         spread_e(0)
         spread_e(1)
-        products(3, 0)
+        products((3,), 0)
         for run in (A, B):
-            quantize_white(run, 2, 1)
+            quantize_white(run, (2,), 1)
         sum_products(2)
 
         for run in (A, B):
-            group_white(run, 3, 0, on_scalar)
-        products(3, 1)
+            group_white(run, (3,), 0, on_scalar)
+        products((3,), 1)
         gram(5, 0)
         reduce_e(2)
         finish(3, 0)
         finish(2, 0)
         gram(4, 0)
-        group_white(A, 3, 1, on_scalar)
-        group_white(B, 3, 1, on_vector)
+        group_white(A, (3,), 1, on_scalar)
         sum_products(3)
         for run in (A, B):
-            quantize_white(run, 3, 0)
-        quantize_white(B, 3, 1)
+            quantize_white(run, (3,), 0)
+        group_white(B, (3,), 1, on_vector)
         reduce_e(3)
-        quantize_white(A, 3, 1)
+        for run in (A, B):
+            quantize_white(run, (3,), 1)
         mirror(1, 0)
         spread_e(2)
         gram(1, 0)

from contextlib import ExitStack

import concourse.mybir as mybir
from concourse.masks import make_identity

C, P, K = 1024, 1024, 1024
FLOPS = 2 * (2 * C * P * K) + 2 * C * C * K

F32 = mybir.dt.float32
BF16 = mybir.dt.bfloat16
U32 = mybir.dt.uint32
U8 = mybir.dt.uint8
FP8 = mybir.dt.float8_e4m3fn
FP8X4 = mybir.dt.float8_e4m3fn_x4
ALU = mybir.AluOpType
COPY = mybir.ActivationFunctionType.Copy

PART = 128
SLOTS = 4
K_PASS = PART * SLOTS
PASSES = P // K_PASS
RUN_LEN = 8
LINE = 4
BANK = 512
BANKS = 8
PAIR = 2 * PART
HALF = C // 2
A, B = 0, 1

V_SLOTS_ON_SCALAR = (2, 1)
WARM_FIRST, WARM_SECOND, WARM_BETWEEN = 4, 7, 2


def tile_crossnobisdissimilaritymatrix_kernel(tc, xa, xb_bytes, xb_scale, v, ca, cb, out):
    nc = tc.nc
    on_vector, on_scalar = nc.vector.tensor_copy, nc.scalar.copy
    with ExitStack() as ctx:
        keep = ctx.enter_context(tc.tile_pool(name="keep", bufs=1))
        work = ctx.enter_context(tc.tile_pool(name="work", bufs=2))
        psum = ctx.enter_context(tc.psum_pool(name="psum", bufs=1))
        ctx.enter_context(tc.manual_schedule())

        made = {}
        opened = []

        def new_bank(shape, dtype=F32):
            tag = "bank%d" % (len(opened) % BANKS)
            opened.append(tag)
            return psum.tile(shape, dtype, name=tag)

        factor_rows = keep.tile([PART, K // SLOTS], BF16, name="factor_rows")
        ident = keep.tile([PART, PART], F32, name="ident")
        warm_in = keep.tile([PART, BANK], BF16, name="warm_in")
        nc.vector.memset(warm_in[:], 0.0)
        nc.vector.memset(factor_rows[:], 0.0)
        make_identity(nc, ident[:])
        ident_bf16 = keep.tile([PART, PART], BF16, name="ident_bf16")
        make_identity(nc, ident_bf16[:])

        scale_cols = keep.tile([PART, P // PART], F32, name="scale_cols")
        scale_spread = keep.tile([PART, P], F32, name="scale_spread")
        ca_cols = keep.tile([PART, PASSES, SLOTS], F32, name="ca_cols")
        cb_cols = keep.tile([PART, PASSES, SLOTS], F32, name="cb_cols")
        e_cols = keep.tile([PART, C // PART], F32, name="e_cols")
        e_spread = keep.tile([PART, C], F32, name="e_spread")
        white_q = {}
        for run in (A, B):
            for h in range(PASSES):
                white_codes = keep.tile([PART, C], U32, name="white_codes_%d_%d" % (run, h), align_bytes=64)
                white_scales = keep.tile([PART, C], U8, name="white_scales_%d_%d" % (run, h), align_bytes=64)
                white_q[run, h] = (white_codes, white_scales)

        def load_scale():
            nc.sync.dma_start(out=scale_cols[:].rearrange("p (b i) -> p b i", i=SLOTS),
                              in_=xb_scale.rearrange("o (b p i) -> (o p) b i", p=PART, i=SLOTS))

        def load_factors():
            for i, factor in enumerate((ca, cb)):
                nc.sync.dma_start(
                    out=factor_rows[SLOTS * i:SLOTS * (i + 1), :].rearrange("s (hq r) -> s hq r", r=RUN_LEN),
                    in_=factor.rearrange("(hq s r) -> s hq r", s=SLOTS, r=RUN_LEN))

        def load_v(g, h):
            raw = keep.tile([PART, SLOTS, K_PASS], BF16, name="v_raw_%d_%d" % (g, h))
            quarter = v[g * K_PASS:(g + 1) * K_PASS, h * K_PASS:(h + 1) * K_PASS]
            nc.sync.dma_start(out=raw[:], in_=quarter.rearrange("(p j) k -> p j k", j=SLOTS))
            made["v_raw", g, h] = raw

        def load_xa(pair):
            raw = keep.tile([PART, 2, P], BF16, name="xa_raw_%d" % pair)
            nc.sync.dma_start(out=raw[:], in_=xa[pair * PAIR:(pair + 1) * PAIR, :].rearrange("(p i) k -> p i k", i=2))
            for i in range(2):
                made["x_rows", A, pair, i] = raw[:, i, :]

        def load_xb(pair):
            raw = keep.tile([PART, 2, P], U8, name="xb_fp8_%d" % pair)
            nc.sync.dma_start(out=raw[:], in_=xb_bytes[pair * PAIR:(pair + 1) * PAIR, :].rearrange("(p i) k -> p i k", i=2))
            made["xb_fp8", pair] = raw

        def spread_scale():
            for b in range(P // BANK):
                bank = new_bank([PART, SLOTS, PART])
                for i in range(SLOTS):
                    col = b * SLOTS + i
                    nc.tensor.transpose(bank[:, i, :], scale_cols[:, col:col + 1].to_broadcast([PART, PART]), ident[:])
                nc.scalar.activation(out=scale_spread[:, b * BANK:(b + 1) * BANK].rearrange("p (m i) -> p m i", i=SLOTS),
                                     in_=bank[:].rearrange("p i m -> p m i"), func=COPY)

        def turn_factors():
            bank = new_bank([PART, PASSES, PART], dtype=BF16)
            for h in range(PASSES):
                nc.tensor.transpose(bank[:, h, :], factor_rows[:, h * PART:(h + 1) * PART], ident_bf16[:])
            nc.scalar.activation(out=ca_cols[:], in_=bank[:, :, 0:SLOTS], func=COPY, scale=-1.0 / P)
            nc.scalar.copy(out=cb_cols[:], in_=bank[:, :, SLOTS:2 * SLOTS])

        def warm(count):
            bank = new_bank([PART, BANK])
            for i in range(count):
                nc.tensor.matmul(bank[:], lhsT=warm_in[:, 0:PART], rhs=warm_in[:], start=True, stop=True)

        def quantize(name, grouped):
            width = grouped.shape[1] // SLOTS
            codes = work.tile([PART, width], U32, name=name + "_codes", align_bytes=64, bufs=4)
            scales = work.tile([PART, width], U8, name=name + "_scales", align_bytes=64, bufs=4)
            nc.vector.quantize_mx(out=codes[:].bitcast(FP8X4), scales=scales[:], in_=grouped)
            return codes, scales

        def mx(acc, stationary, s_cols, moving, m_cols, start, stop):
            nc.tensor.matmul_mx(
                out=acc, lhsT=stationary[0][:, s_cols].bitcast(FP8X4), lhsT_scale=stationary[1][:, s_cols],
                rhs=moving[0][:, m_cols].bitcast(FP8X4), rhs_scale=moving[1][:, m_cols], start=start, stop=stop)

        def group_v(g, h, scalar_slots):
            grouped = work.tile([PART, SLOTS, PART * SLOTS], BF16, name="v_grouped", align_bytes=64)
            cut = SLOTS - scalar_slots
            source = made["v_raw", g, h][:].rearrange("p j (q s r) -> p s q j r", s=SLOTS, r=RUN_LEN)
            target = grouped[:].rearrange("p s (q r j) -> p s q j r", r=RUN_LEN, j=SLOTS)
            on_vector(out=target[:, 0:cut], in_=source[:, 0:cut])
            if scalar_slots:
                on_scalar(out=target[:, cut:SLOTS], in_=source[:, cut:SLOTS])
            made["v_grouped", g, h] = grouped

        def quantize_v(g, h):
            made["v_q", g, h] = quantize("v", made["v_grouped", g, h][:].rearrange("p s c -> p (s c)"))

        def widen_xb(pair):
            for i in range(2):
                rows = work.tile([PART, P], BF16, name="xb_rows", bufs=4)
                nc.vector.tensor_tensor(out=rows[:], in0=made["xb_fp8", pair][:, i, :].bitcast(FP8),
                                        in1=scale_spread[:], op=ALU.mult)
                made["x_rows", B, pair, i] = rows[:]

        def turn_x(run, pair):
            half, second = divmod(pair, 2)
            words_a_pass = K_PASS // 2
            for g in range(PASSES):
                if not second:
                    made["x_grouped", run, half, g] = work.tile([PART, HALF * SLOTS], BF16, name="x_grouped", align_bytes=64, bufs=4)
                bank = new_bank([PART, 2, PAIR])
                for i in range(2):
                    words = made["x_rows", run, pair, i].bitcast(F32)
                    for u in range(2):
                        nc.tensor.transpose(bank[:, u, i * PART:(i + 1) * PART],
                                            words[:, words_a_pass * g + u:words_a_pass * (g + 1):2], ident[:])
                cols = slice(second * PAIR * SLOTS, (second + 1) * PAIR * SLOTS)
                nc.scalar.copy(out=made["x_grouped", run, half, g][:, cols].bitcast(F32).rearrange("p (m i u) -> p m i u", i=2, u=2),
                               in_=bank[:].rearrange("p u (i m) -> p m i u", i=2))

        def quantize_x(run, half, g):
            made["x_q", run, half, g] = quantize("x", made["x_grouped", run, half, g][:])

        def whiten(run, half, h):
            white = work.tile([PART, SLOTS, HALF], F32, name="white", bufs=6)
            for s in range(SLOTS):
                bank = new_bank([PART, HALF])
                for g in range(PASSES):
                    mx(bank[:], made["v_q", g, h], slice(s * PART, (s + 1) * PART), made["x_q", run, half, g], slice(0, HALF),
                       g == 0, g == PASSES - 1)
                nc.scalar.activation(out=white[:, s, :], in_=bank[:], func=COPY, scale=(ca_cols, cb_cols)[run][:, h, s:s + 1])
            made["white", run, half, h] = white

        def white_cols(run, pairs, h):
            half, second = divmod(pairs[0], 2)
            return made["white", run, half, h][:, :, second * PAIR:(second + len(pairs)) * PAIR]

        def group_white(run, pairs, h, copy):
            grouped = work.tile([PART, len(pairs) * PAIR, SLOTS], BF16, name="white_grouped", align_bytes=64, bufs=3)
            copy(out=grouped[:].rearrange("p (c i) s -> p c s i", i=LINE),
                 in_=white_cols(run, pairs, h).rearrange("p s (c i) -> p c s i", i=LINE))
            made["white_grouped", run, pairs, h] = grouped

        def quantize_white(run, pairs, h):
            cols = slice(pairs[0] * PAIR, (pairs[-1] + 1) * PAIR)
            codes, scales = white_q[run, h]
            nc.vector.quantize_mx(out=codes[:, cols].bitcast(FP8X4), scales=scales[:, cols],
                                  in_=made["white_grouped", run, pairs, h][:].rearrange("p c s -> p (c s)"))

        def products(pairs, h):
            prod = work.tile([PART, SLOTS, len(pairs) * PAIR], F32, name="prod", bufs=3)
            nc.vector.tensor_tensor(out=prod[:], in0=white_cols(A, pairs, h), in1=white_cols(B, pairs, h), op=ALU.mult)
            for n, pair in enumerate(pairs):
                made["prod", pair, h] = prod[:, :, n * PAIR:(n + 1) * PAIR]

        def sum_products(pair):
            bank = new_bank([PART, 2, PART])
            for i in range(2):
                for h in range(PASSES):
                    for s in range(SLOTS):
                        nc.tensor.matmul(bank[:, i, :], lhsT=made["prod", pair, h][:, s, i * PART:(i + 1) * PART], rhs=ident[:],
                                         is_transpose=True, start=(h == 0 and s == 0), stop=(h == PASSES - 1 and s == SLOTS - 1))
            made["e_bank", pair] = bank

        def reduce_e(pair):
            nc.vector.tensor_reduce(out=e_cols[:, 2 * pair:2 * pair + 2], in_=made["e_bank", pair][:],
                                    axis=mybir.AxisListType.X, op=ALU.add)

        def spread_e(pair):
            bank = new_bank([PART, 2, PART])
            for i in range(2):
                col = 2 * pair + i
                nc.tensor.transpose(bank[:, i, :], e_cols[:, col:col + 1].to_broadcast([PART, PART]), ident[:])
            nc.scalar.copy(out=e_spread[:, pair * PAIR:(pair + 1) * PAIR], in_=bank[:].rearrange("p i m -> p (i m)"))

        def out_cols(tile, half):
            return slice(half * HALF, min((half + 1) * HALF, (tile // 2 + 1) * PAIR))

        def gram(tile, half):
            cols = out_cols(tile, half)
            bank = new_bank([PART, cols.stop - cols.start])
            for h in range(PASSES):
                for run in (A, B):
                    mx(bank[:], white_q[run, h], slice(tile * PART, (tile + 1) * PART), white_q[1 - run, h], cols,
                       h == 0 and run == A, h == PASSES - 1 and run == B)
            made["gram", tile, half] = bank

        def finish(tile, half):
            cols = out_cols(tile, half)
            rows = keep.tile([PART, cols.stop - cols.start], F32, name="rows_%d_%d" % (tile, half))
            nc.vector.scalar_tensor_tensor(out=rows[:], in0=made["gram", tile, half][:], scalar=e_cols[:, tile:tile + 1],
                                           in1=e_spread[:, cols], op0=ALU.subtract, op1=ALU.subtract)
            nc.sync.dma_start(out=out[tile * PART:(tile + 1) * PART, cols], in_=rows[:])
            made["rows", tile, half] = rows

        def mirror(pair, earlier):
            half, second = divmod(earlier, 2)
            bank = new_bank([PART, 2, PAIR])
            for j in range(2):
                c0 = second * PAIR + j * PART
                for i in range(2):
                    nc.tensor.transpose(bank[:, j, i * PART:(i + 1) * PART],
                                        made["rows", 2 * pair + i, half][:, c0:c0 + PART], ident[:])
            mirrored = work.tile([PART, 2, PAIR], F32, name="mirrored", bufs=5)
            nc.scalar.copy(out=mirrored[:], in_=bank[:])
            target = out[earlier * PAIR:(earlier + 1) * PAIR, pair * PAIR:(pair + 1) * PAIR]
            nc.sync.dma_start(out=target.rearrange("(j p) c -> p j c", p=PART), in_=mirrored[:])

        load_scale()
        load_v(0, 0)
        load_xb(0)
        load_xa(0)
        load_factors()
        load_xb(1)
        load_v(1, 0)
        load_xa(1)
        load_xb(2)
        load_xa(2)
        load_v(0, 1)
        load_xa(3)
        load_xb(3)
        load_v(1, 1)

        warm(WARM_FIRST)
        spread_scale()
        warm(WARM_SECOND)
        group_v(0, 0, V_SLOTS_ON_SCALAR[0])
        turn_factors()
        turn_x(A, 0)
        widen_xb(0)
        turn_x(B, 0)
        widen_xb(1)
        group_v(1, 0, V_SLOTS_ON_SCALAR[1])
        warm(WARM_BETWEEN)
        turn_x(A, 1)
        turn_x(B, 1)
        warm(WARM_BETWEEN)
        for g in range(PASSES):
            quantize_v(g, 0)
            quantize_x(A, 0, g)
        turn_x(A, 2)

        whiten(A, 0, 0)
        for g in range(PASSES):
            quantize_x(B, 0, g)
        whiten(B, 0, 0)
        for g in range(PASSES):
            group_v(g, 1, 0)
        for g in range(PASSES):
            quantize_v(g, 1)
        whiten(A, 0, 1)
        widen_xb(2)
        turn_x(A, 3)
        turn_x(B, 2)
        widen_xb(3)
        whiten(B, 0, 1)
        for g in range(PASSES):
            quantize_x(A, 1, g)
        turn_x(B, 3)

        first_half = (0, 1)
        products(first_half, 0)
        whiten(A, 1, 0)
        group_white(A, first_half, 0, on_vector)
        for g in range(PASSES):
            quantize_x(B, 1, g)
        whiten(B, 1, 0)
        group_white(B, first_half, 0, on_vector)
        products(first_half, 1)
        whiten(A, 1, 1)
        for run in (A, B):
            quantize_white(run, first_half, 0)
        for run in (B, A):
            group_white(run, first_half, 1, on_vector)
        whiten(B, 1, 1)
        for pair in first_half:
            sum_products(pair)
        products((2,), 0)
        for run in (B, A):
            quantize_white(run, first_half, 1)

        reduce_e(0)
        for run in (A, B):
            group_white(run, (2,), 0, on_scalar)
        gram(3, 0)
        gram(2, 0)
        reduce_e(1)
        products((2,), 1)
        for run in (A, B):
            quantize_white(run, (2,), 0)
        for run in (A, B):
            group_white(run, (2,), 1, on_scalar)
        spread_e(0)
        spread_e(1)
        products((3,), 0)
        for run in (A, B):
            quantize_white(run, (2,), 1)
        sum_products(2)

        for run in (A, B):
            group_white(run, (3,), 0, on_scalar)
        products((3,), 1)
        gram(5, 0)
        reduce_e(2)
        finish(3, 0)
        finish(2, 0)
        gram(4, 0)
        group_white(A, (3,), 1, on_scalar)
        sum_products(3)
        for run in (A, B):
            quantize_white(run, (3,), 0)
        group_white(B, (3,), 1, on_vector)
        reduce_e(3)
        for run in (A, B):
            quantize_white(run, (3,), 1)
        mirror(1, 0)
        spread_e(2)
        gram(1, 0)
        for tile in (5, 4, 1):
            finish(tile, 0)

        for tile in (7, 6):
            gram(tile, 0)
        for tile in (7, 6):
            finish(tile, 0)
        spread_e(3)
        for pair in (2, 3):
            for earlier in (0, 1):
                mirror(pair, earlier)
        for tile in (7, 6, 5, 4):
            gram(tile, 1)
        for tile in (7, 6, 5, 4):
            finish(tile, 1)
        mirror(3, 2)
        gram(0, 0)
        finish(0, 0)
